import numpy as np
import ml_dtypes


def mxq(x, axis, fmt="e4m3"):
    dtype, down = {"e4m3": (ml_dtypes.float8_e4m3fn, 7), "e5m2": (ml_dtypes.float8_e5m2, 14)}[fmt]
    v = np.moveaxis(np.asarray(x, np.float32).astype(ml_dtypes.bfloat16).astype(np.float64), axis, -1)
    blocks = v.reshape(v.shape[:-1] + (-1, 32))
    amax = np.abs(blocks).max(-1, keepdims=True)
    byte = np.maximum(np.where(amax > 0, np.frexp(amax)[1] - 1 + 127, 0) - down, 1)
    scale = np.exp2(byte - 127.0)
    codes = (blocks / scale).astype(np.float32).astype(dtype).astype(np.float64)
    return np.moveaxis((codes * scale).reshape(v.shape), -1, axis)


WIDE = False


def mx_kscale(k):
    if not WIDE:
        return np.ones(k)
    levels = np.array([10, -10, 5, -5, 0])
    if k % 512:
        return np.exp2(np.random.permutation(np.resize(levels, k // 32))).repeat(32)
    a = np.empty((k // 512, 16))
    for p in range(k // 512):
        a[p, :8] = np.random.permutation(np.resize(levels, 8))
        for g in range(8):
            far = levels[np.abs(levels - a[p, g]) >= 10]
            a[p, g + 8] = far[np.random.randint(len(far))]
    return np.exp2(a.ravel()).repeat(32)


def f64(x):
    return np.asarray(x).astype(np.float64)


def striped(idx):
    return np.tile(idx.reshape(-1, 16).T, (8, 1)).astype(np.uint16)


def unstriped(offs):
    return offs[:16].T.reshape(-1).astype(np.int64)


E2M1 = np.array([0.0, 0.5, 1.0, 1.5, 2.0, 3.0, 4.0, 6.0, -0.0, -0.5, -1.0, -1.5, -2.0, -3.0, -4.0, -6.0])


def pack_weight(w, fmt):
    k, n = w.shape
    w = f64(np.asarray(w, np.float32).astype(ml_dtypes.bfloat16)).reshape(k // 32, 32, n)
    amax = np.abs(w).max(1)
    if fmt == "e4m3":
        byte = np.frexp(amax)[1] - 1 + 127 - 7
    else:
        mant, ex = np.frexp(amax / 6.0)
        byte = np.where(mant > 0.5, ex, ex - 1) + 127
    byte = np.clip(np.where(amax > 0, byte, 1), 1, 254)
    scaled = (w * np.exp2(127.0 - byte)[:, None, :]).reshape(k, n).astype(np.float32)
    by_word = np.ascontiguousarray(scaled.reshape(k // 512, 128, 4, n).transpose(0, 1, 3, 2))
    if fmt == "e4m3":
        words = by_word.astype(ml_dtypes.float8_e4m3fn).view(np.uint8)
    else:
        c = by_word.astype(ml_dtypes.float4_e2m1fn).view(np.uint8) & 0xF
        words = (c[..., 0::2] | (c[..., 1::2] << 4)).reshape(k // 512, 128, 2 * n)
    return np.ascontiguousarray(words), np.ascontiguousarray(byte.astype(np.uint8).reshape(k // 512, 16, n))


def unpack_weight(words, scales, fmt):
    g, _, n = scales.shape
    words = np.ascontiguousarray(words).reshape(g, 128, n, -1)
    if fmt == "e4m3":
        vals = words.view(ml_dtypes.float8_e4m3fn).astype(np.float64)
    else:
        nib = np.empty((g, 128, n, 4), np.uint8)
        nib[..., 0::2] = words & 0xF
        nib[..., 1::2] = words >> 4
        vals = E2M1[nib]
    vals = vals * np.repeat(np.exp2(scales.astype(np.float64) - 127.0), 8, axis=1)[..., None]
    return vals.transpose(0, 1, 3, 2).reshape(g * 512, n)


def relu2(v):
    return np.maximum(v, 0.0) ** 2


K, T, E, C, H, N = 1024, 2048, 8, 128, 512, 128


def by_expert(wq, xq):
    return np.concatenate([wq[e].T @ xq[:, e * C:(e + 1) * C] for e in range(E)], axis=1)


def setup_inputs():
    n = np.random.standard_normal
    s = mx_kscale(K)[:, None]
    u = mx_kscale(H)
    w1 = [pack_weight(m, "e2m1") for m in n((E, K, H)) / np.sqrt(K) / s[None] * u[None, None, :]]
    w2 = [pack_weight(m, "e2m1") for m in n((E, H, N)) / np.sqrt(H) / u[None, :, None] ** 2]
    return {
        "xT": (n((K, T)) * s).astype(np.float32),
        "w1_words": np.stack([m[0] for m in w1]),
        "w1_scales": np.stack([m[1] for m in w1]),
        "w2_words": np.stack([m[0] for m in w2]),
        "w2_scales": np.stack([m[1] for m in w2]),
        "gate": np.tile(np.random.uniform(0.2, 1.0, E * C), (N, 1)).astype(np.float32),
        "offs": striped(np.random.permutation(T)[:E * C]),
    }


def reference(xT, w1_words, w1_scales, w2_words, w2_scales, gate, offs):
    idx = unstriped(offs)
    w1 = np.stack([unpack_weight(w1_words[e], w1_scales[e], "e2m1") for e in range(E)])
    w2 = np.stack([unpack_weight(w2_words[e], w2_scales[e], "e2m1") for e in range(E)])
    xq = mxq(f64(xT)[:, idx], 0, "e4m3")
    h = relu2(by_expert(w1, xq))
    y = by_expert(w2, mxq(h, 0, "e4m3"))
    out = np.zeros((N, T))
    out[:, idx] = f64(gate) * y
    return out

@@ -1,0 +1,210 @@
+from contextlib import ExitStack
+
+import concourse.mybir as mybir
+from concourse.masks import make_identity
+
+K, T, E, C, H, N = 1024, 2048, 8, 128, 512, 128
+SLOTS = E * C
+FLOPS = 2 * SLOTS * (K * H + H * N)
+
+F32 = mybir.dt.float32
+BF16 = mybir.dt.bfloat16
+I32 = mybir.dt.int32
+U32 = mybir.dt.uint32
+U16 = mybir.dt.uint16
+U8 = mybir.dt.uint8
+FP8X4 = mybir.dt.float8_e4m3fn_x4
+FP4X4 = mybir.dt.float4_e2m1fn_x4
+ACT = mybir.ActivationFunctionType
+MULT = mybir.AluOpType.mult
+
+P = 128
+PASSES = K // 512
+GROUP = 256
+GROUPS = SLOTS // GROUP
+FIRST = 4
+
+CHUNKS = (
+    (0, 0, 256, 128),
+    (0, 256, 256, 96),
+    (0, 512, 512, 192),
+    (0, 1024, 512, 192),
+    (0, 1536, 512, 192),
+    (1, 0, 512, 64),
+    (1, 512, 512, 64),
+    (1, 1024, 512, 96),
+    (1, 1536, 256, 96),
+    (1, 1792, 256, 160),
+)
+
+
+def tile_moe_pln_mlp_relu2_kernel(tc, xT, w1_words, w1_scales, w2_words, w2_scales, gate, offs, out):
+    nc = tc.nc
+    with ExitStack() as ctx:
+        lists = ctx.enter_context(tc.tile_pool(name="lists", bufs=1))
+        held = ctx.enter_context(tc.tile_pool(name="held", bufs=1))
+        psum_v = ctx.enter_context(tc.psum_pool(name="psum_v", bufs=3))
+        psum_t = ctx.enter_context(tc.psum_pool(name="psum_t", bufs=3))
+        psum_y = ctx.enter_context(tc.psum_pool(name="psum_y", bufs=2))
+
+        offsets = lists.tile([P, SLOTS // 16], U16, name="offsets")
+
+        raws = []
+        for i, (s, t0, width, by_vector) in enumerate(CHUNKS):
+            raw = held.tile([P, 4, width], F32, name=f"raw{i}")
+            nc.sync.dma_start(out=raw[:], in_=xT[512 * s : 512 * (s + 1), t0 : t0 + width].rearrange("(p j) w -> p j w", j=4))
+            raws.append(raw)
+            if i == 0:
+                nc.sync.dma_start(offsets[:], offs)
+
+        w1s = held.tile([P, E * PASSES * H], U8, name="w1s", align_bytes=64)
+        w2s = held.tile([P, E * N], U8, name="w2s", align_bytes=64)
+        out_sb = held.tile([P, T], F32, name="out_sb", align_bytes=64)
+        nc.vector.memset(w1s[:].bitcast(I32), 0)
+        nc.vector.memset(out_sb[:], 0.0)
+        bytes_all = [held.tile([P, T], U8, name=f"bytes_all{s}", align_bytes=64) for s in range(PASSES)]
+        nc.gpsimd.memset(bytes_all[0][:], 0)
+        nc.gpsimd.memset(w2s[:].bitcast(I32), 0)
+        ident = held.tile([P, P], F32, name="ident")
+        make_identity(nc, ident[:])
+        nc.gpsimd.memset(bytes_all[1][:], 0)
+        warm = held.tile([P, 1], F32, name="warm")
+        warm_in = held.tile([P, 1], F32, name="warm_in")
+        nc.vector.memset(warm_in[:], 0.0)
+        nc.scalar.activation(out=warm[:], in_=warm_in[:], func=ACT.Square)
+
+        w1w = [held.tile([P, 2 * PASSES * 2 * H], U8, name=f"w1w{g}", align_bytes=64) for g in range(GROUPS)]
+        w2w = held.tile([P, E * 2 * N], U8, name="w2w", align_bytes=64)
+        gate_sb = held.tile([P, SLOTS], F32, name="gate_sb", align_bytes=64)
+
+        w1_int = w1_words.bitcast(I32).rearrange("(g e) s p b -> g p (e s) b", e=2)
+        w1s_int = w1_scales.bitcast(I32).rearrange("e s (q r) b -> r q (e s) b", r=4)
+        w2s_int = w2_scales.bitcast(I32).rearrange("e o (q r) b -> r q (e o) b", r=4)
+
+        def load_w1(g):
+            nc.sync.dma_start(out=w1w[g][:].bitcast(I32).rearrange("p (e b) -> p e b", e=2 * PASSES), in_=w1_int[g])
+
+        w1s_view = w1s[:].bitcast(I32).rearrange("p (e b) -> p e b", e=E * PASSES)
+
+        def load_w1_scales(a, b):
+            for r in range(4):
+                nc.sync.dma_start(out=w1s_view[r:P:32, a:b, :], in_=w1s_int[r][:, a:b, :])
+
+        load_w1_scales(0, FIRST)
+        load_w1(0)
+        load_w1_scales(FIRST, E * PASSES)
+        load_w1(1)
+        nc.sync.dma_start(
+            out=w2w[:].bitcast(I32).rearrange("p (e b) -> p e b", e=E),
+            in_=w2_words.bitcast(I32).rearrange("e o p b -> p (e o) b"),
+        )
+        w2s_view = w2s[:].bitcast(I32).rearrange("p (e b) -> p e b", e=E)
+        for r in range(4):
+            nc.sync.dma_start(out=w2s_view[r:P:32], in_=w2s_int[r])
+        nc.sync.dma_start(out=gate_sb[:], in_=gate)
+        load_w1(2)
+        load_w1(3)
+
+        words_all = [held.tile([P, T], U32, name=f"words_all{s}", align_bytes=64) for s in range(PASSES)]
+        words = [held.tile([P, SLOTS], U32, name=f"words{s}", align_bytes=64) for s in range(PASSES)]
+        scales = [held.tile([P, SLOTS], U8, name=f"scales{s}", align_bytes=64) for s in range(PASSES)]
+
+        def gather(s, a, b):
+            picked = offsets[:, a // 16 : b // 16]
+            nc.vector.tensor_copy(words[s][:, a:b], words_all[s][:].indirect(picked))
+            nc.vector.tensor_copy(scales[s][:, a:b], bytes_all[s][:].indirect(picked))
+
+        for i, (s, t0, width, by_vector) in enumerate(CHUNKS):
+            piece = held.tile([P, width, 4], BF16, name=f"piece{i}", align_bytes=64)
+            for a, b, mover in ((0, by_vector, "v"), (by_vector, width, "s")):
+                if a == b:
+                    continue
+                dst = piece[:, a:b, :].rearrange("p (c i) t -> p c t i", i=4)
+                src = raws[i][:, :, a:b].rearrange("p t (c i) -> p c t i", i=4)
+                if mover == "v":
+                    nc.vector.tensor_copy(dst, src)
+                else:
+                    nc.scalar.activation(out=dst, in_=src, func=ACT.Copy)
+            nc.vector.quantize_mx(
+                out=words_all[s][:, t0 : t0 + width].bitcast(FP8X4),
+                scales=bytes_all[s][:, t0 : t0 + width],
+                in_=piece[:].rearrange("p w t -> p (w t)"),
+            )
+            if s == 0 and t0 + width == T:
+                gather(0, 0, SLOTS)
+
+        for a, b in ((0, 256), (256, 512), (512, 1024)):
+            gather(PASSES - 1, a, b)
+
+        y_sb = held.tile([P, SLOTS], F32, name="y_sb", align_bytes=64)
+        v, r, turned, h, h_words, h_scales, y = {}, {}, {}, {}, {}, {}, {}
+
+        def first_layer(e):
+            g, half = divmod(e, 2)
+            slots = slice(e * C, (e + 1) * C)
+            v[e] = psum_v.tile([C, H], F32, name="v")
+            for s in range(PASSES):
+                at = (half * PASSES + s) * 2 * H
+                sc = (e * PASSES + s) * H
+                nc.tensor.matmul_mx(
+                    out=v[e][:],
+                    lhsT=words[s][:, slots].bitcast(FP8X4),
+                    lhsT_scale=scales[s][:, slots],
+                    rhs=w1w[g][:, at : at + 2 * H].bitcast(FP4X4),
+                    rhs_scale=w1s[:, sc : sc + H],
+                    start=(s == 0),
+                    stop=(s == PASSES - 1),
+                )
+
+        def relu(e):
+            r[e] = held.tile([C, 4, P], F32, name=f"r{e}")
+            nc.scalar.activation(out=r[e][:], in_=v[e][:].rearrange("c (p t) -> c t p", t=4), func=ACT.Relu)
+
+        def turn(e):
+            turned[e] = psum_t.tile([P, 4, C], F32, name="turned")
+            for t in range(4):
+                nc.tensor.transpose(turned[e][:, t, :], r[e][:, t, :], ident[:])
+
+        def square(e):
+            h[e] = held.tile([P, C, 4], BF16, name=f"h{e}", align_bytes=64)
+            nc.scalar.activation(out=h[e][:], in_=turned[e][:].rearrange("p t c -> p c t"), func=ACT.Square)
+
+        def quantise(e):
+            h_words[e] = held.tile([P, C], U32, name=f"h_words{e}", align_bytes=64)
+            h_scales[e] = held.tile([P, C], U8, name=f"h_scales{e}", align_bytes=64)
+            nc.vector.quantize_mx(out=h_words[e][:].bitcast(FP8X4), scales=h_scales[e][:], in_=h[e][:].rearrange("p c t -> p (c t)"))
+
+        def second_layer(e):
+            g, half = divmod(e, 2)
+            if half == 0:
+                y[g] = psum_y.tile([N, 2 * C], F32, name="y")
+            nc.tensor.matmul_mx(
+                out=y[g][:, half * C : (half + 1) * C],
+                lhsT=w2w[:, e * 2 * N : (e + 1) * 2 * N].bitcast(FP4X4),
+                lhsT_scale=w2s[:, e * N : (e + 1) * N],
+                rhs=h_words[e][:].bitcast(FP8X4),
+                rhs_scale=h_scales[e][:],
+                start=True,
+                stop=True,
+            )
+
+        def put_back(g):
+            cols = slice(g * GROUP, (g + 1) * GROUP)
+            nc.scalar.copy(y_sb[:, cols], y[g][:])
+            picked = offsets[:, g * GROUP // 16 : (g + 1) * GROUP // 16]
+            nc.vector.tensor_tensor(out_sb[:].indirect(picked), y_sb[:, cols], gate_sb[:, cols], MULT)
+
+        for k in range(E + 3):
+            if k < E:
+                first_layer(k)
+                relu(k)
+            if 0 <= k - 1 < E:
+                turn(k - 1)
+                square(k - 1)
+            if 0 <= k - 2 < E:
+                quantise(k - 2)
+            if 0 <= k - 3 < E:
+                second_layer(k - 3)
+                if k % 2 == 0:
+                    put_back((k - 3) // 2)
+        nc.sync.dma_start(out=out, in_=out_sb[:])

@@ -22,19 +22,20 @@ P = 128
 PASSES = K // 512
 GROUP = 256
 GROUPS = SLOTS // GROUP
-FIRST = 4
+
+SCALE_GROUPS = ((0, 2), (2, 5), (5, 8))
 
 CHUNKS = (
-    (0, 0, 256, 128),
-    (0, 256, 256, 96),
-    (0, 512, 512, 192),
-    (0, 1024, 512, 192),
-    (0, 1536, 512, 192),
-    (1, 0, 512, 64),
-    (1, 512, 512, 64),
-    (1, 1024, 512, 96),
+    (0, 0, 256, 96),
+    (0, 256, 512, 160),
+    (0, 768, 512, 160),
+    (0, 1280, 512, 192),
+    (0, 1792, 256, 160),
+    (1, 0, 512, 0),
+    (1, 512, 512, 0),
+    (1, 1024, 512, 160),
     (1, 1536, 256, 96),
-    (1, 1792, 256, 160),
+    (1, 1792, 256, 144),
 )
 
 
@@ -43,67 +44,59 @@ def tile_moe_pln_mlp_relu2_kernel(tc, xT, w1_words, w1_scales, w2_words, w2_scal
     with ExitStack() as ctx:
         lists = ctx.enter_context(tc.tile_pool(name="lists", bufs=1))
         held = ctx.enter_context(tc.tile_pool(name="held", bufs=1))
-        psum_v = ctx.enter_context(tc.psum_pool(name="psum_v", bufs=3))
-        psum_t = ctx.enter_context(tc.psum_pool(name="psum_t", bufs=3))
-        psum_y = ctx.enter_context(tc.psum_pool(name="psum_y", bufs=2))
+        psum = ctx.enter_context(tc.psum_pool(name="psum", bufs=1))
+        banks = [psum.tile([P, 512], F32, name=f"bank{b}") for b in range(7)]
 
         offsets = lists.tile([P, SLOTS // 16], U16, name="offsets")
 
         raws = []
         for i, (s, t0, width, by_vector) in enumerate(CHUNKS):
-            raw = held.tile([P, 4, width], F32, name=f"raw{i}")
+            raw = held.tile([P, 4, width], F32, name=f"raw{i}", tag=f"slot{i}", align_bytes=64)
             nc.sync.dma_start(out=raw[:], in_=xT[512 * s : 512 * (s + 1), t0 : t0 + width].rearrange("(p j) w -> p j w", j=4))
             raws.append(raw)
             if i == 0:
                 nc.sync.dma_start(offsets[:], offs)
+                gate_cols = held.tile([P, SLOTS // P], F32, name="gate_cols")
+                nc.sync.dma_start(out=gate_cols[:], in_=gate[0].rearrange("(p j) -> p j", p=P))
 
-        w1s = held.tile([P, E * PASSES * H], U8, name="w1s", align_bytes=64)
-        w2s = held.tile([P, E * N], U8, name="w2s", align_bytes=64)
+        w1s, w1w, w2w = {}, {}, {}
+
+        def zero_w1_scales(a, engine, tag):
+            first, last = SCALE_GROUPS[a]
+            w1s[a] = held.tile([P, (last - first) * PASSES * H], U8, name=f"w1s{a}", tag=tag, align_bytes=64)
+            engine.memset(w1s[a][:].bitcast(I32), 0)
+
         out_sb = held.tile([P, T], F32, name="out_sb", align_bytes=64)
-        nc.vector.memset(w1s[:].bitcast(I32), 0)
-        nc.vector.memset(out_sb[:], 0.0)
         bytes_all = [held.tile([P, T], U8, name=f"bytes_all{s}", align_bytes=64) for s in range(PASSES)]
-        nc.gpsimd.memset(bytes_all[0][:], 0)
-        nc.gpsimd.memset(w2s[:].bitcast(I32), 0)
-        ident = held.tile([P, P], F32, name="ident")
-        make_identity(nc, ident[:])
-        nc.gpsimd.memset(bytes_all[1][:], 0)
         warm = held.tile([P, 1], F32, name="warm")
         warm_in = held.tile([P, 1], F32, name="warm_in")
         nc.vector.memset(warm_in[:], 0.0)
         nc.scalar.activation(out=warm[:], in_=warm_in[:], func=ACT.Square)
+        zero_w1_scales(0, nc.gpsimd, "w1s0")
+        zero_w1_scales(1, nc.gpsimd, "w1s1")
+        for s in range(PASSES):
+            nc.vector.memset(bytes_all[s][:].bitcast(I32), 0)
+        ident = held.tile([P, P], F32, name="ident")
+        make_identity(nc, ident[:])
 
-        w1w = [held.tile([P, 2 * PASSES * 2 * H], U8, name=f"w1w{g}", align_bytes=64) for g in range(GROUPS)]
-        w2w = held.tile([P, E * 2 * N], U8, name="w2w", align_bytes=64)
-        gate_sb = held.tile([P, SLOTS], F32, name="gate_sb", align_bytes=64)
-
-        w1_int = w1_words.bitcast(I32).rearrange("(g e) s p b -> g p (e s) b", e=2)
+        w1_int = w1_words.bitcast(I32).rearrange("e s p b -> e p s b")
         w1s_int = w1_scales.bitcast(I32).rearrange("e s (q r) b -> r q (e s) b", r=4)
         w2s_int = w2_scales.bitcast(I32).rearrange("e o (q r) b -> r q (e o) b", r=4)
 
-        def load_w1(g):
-            nc.sync.dma_start(out=w1w[g][:].bitcast(I32).rearrange("p (e b) -> p e b", e=2 * PASSES), in_=w1_int[g])
+        def load_w1(e, tag):
+            w1w[e] = held.tile([P, PASSES * 2 * H], U8, name=f"w1w{e}", tag=tag, align_bytes=64)
+            nc.sync.dma_start(out=w1w[e][:].bitcast(I32).rearrange("p (s b) -> p s b", s=PASSES), in_=w1_int[e])
 
-        w1s_view = w1s[:].bitcast(I32).rearrange("p (e b) -> p e b", e=E * PASSES)
-
-        def load_w1_scales(a, b):
+        def load_w1_scales(a):
+            first, last = SCALE_GROUPS[a]
+            view = w1s[a][:].bitcast(I32).rearrange("p (e b) -> p e b", e=(last - first) * PASSES)
             for r in range(4):
-                nc.sync.dma_start(out=w1s_view[r:P:32, a:b, :], in_=w1s_int[r][:, a:b, :])
+                nc.sync.dma_start(out=view[r:P:32], in_=w1s_int[r][:, first * PASSES : last * PASSES, :])
 
-        load_w1_scales(0, FIRST)
-        load_w1(0)
-        load_w1_scales(FIRST, E * PASSES)
-        load_w1(1)
-        nc.sync.dma_start(
-            out=w2w[:].bitcast(I32).rearrange("p (e b) -> p e b", e=E),
-            in_=w2_words.bitcast(I32).rearrange("e o p b -> p (e o) b"),
-        )
-        w2s_view = w2s[:].bitcast(I32).rearrange("p (e b) -> p e b", e=E)
-        for r in range(4):
-            nc.sync.dma_start(out=w2s_view[r:P:32], in_=w2s_int[r])
-        nc.sync.dma_start(out=gate_sb[:], in_=gate)
-        load_w1(2)
-        load_w1(3)
+        for a in range(2):
+            load_w1_scales(a)
+            for e in range(*SCALE_GROUPS[a]):
+                load_w1(e, f"w1w{e}")
 
         words_all = [held.tile([P, T], U32, name=f"words_all{s}", align_bytes=64) for s in range(PASSES)]
         words = [held.tile([P, SLOTS], U32, name=f"words{s}", align_bytes=64) for s in range(PASSES)]
@@ -133,78 +126,134 @@ def tile_moe_pln_mlp_relu2_kernel(tc, xT, w1_words, w1_scales, w2_words, w2_scal
             if s == 0 and t0 + width == T:
                 gather(0, 0, SLOTS)
 
-        for a, b in ((0, 256), (256, 512), (512, 1024)):
-            gather(PASSES - 1, a, b)
+        half = E // 2
+        w2_int = w2_words.bitcast(I32).rearrange("(a e) o p b -> a p (e o) b", a=2)
 
-        y_sb = held.tile([P, SLOTS], F32, name="y_sb", align_bytes=64)
-        v, r, turned, h, h_words, h_scales, y = {}, {}, {}, {}, {}, {}, {}
+        def load_w2(a, tag):
+            w2w[a] = held.tile([P, half * 2 * N], U8, name=f"w2w{a}", tag=tag, align_bytes=64)
+            nc.sync.dma_start(out=w2w[a][:].bitcast(I32).rearrange("p (e b) -> p e b", e=half), in_=w2_int[a])
+
+        w2s = held.tile([P, E * N], U8, name="w2s", tag="slot0", align_bytes=64)
+        nc.vector.memset(w2s[:].bitcast(I32), 0)
+        w2s_view = w2s[:].bitcast(I32).rearrange("p (e b) -> p e b", e=E)
+        for r in range(4):
+            nc.sync.dma_start(out=w2s_view[r:P:32], in_=w2s_int[r])
+        load_w2(0, "slot1")
+        zero_w1_scales(2, nc.vector, "slot2")
+        load_w1_scales(2)
+        load_w1(5, "slot3")
+        load_w1(6, "slot4")
+        load_w1(7, "slot5")
+        load_w2(1, "slot6")
+
+        gate_sb = held.tile([P, SLOTS], F32, name="gate_sb", align_bytes=64)
+        for a in range(2):
+            for j in range(4):
+                column = gate_cols[:, 4 * a + j : 4 * a + j + 1].to_broadcast([P, P])
+                nc.tensor.transpose(banks[a][:, j * P : (j + 1) * P], column, ident[:])
+            nc.scalar.copy(
+                gate_sb[:].rearrange("q (p a j) -> q a p j", a=2, j=4)[:, a],
+                banks[a][:].rearrange("q (j p) -> q p j", j=4),
+            )
+
+        for a in range(0, T, 512):
+            nc.vector.memset(out_sb[:, a : a + 512], 0.0)
+
+        for g in range(GROUPS):
+            gather(PASSES - 1, g * GROUP, (g + 1) * GROUP)
+
+        v_bank = (0, 1, 0, 1, 0, 2, 0, 4)
+        turned_bank = (2, 3, 2, 3, 4, 3, 5, 3)
+        y_bank = (1, 2, 4, 6)
+        r = [held.tile([C, 4, P], F32, name=f"r{e}") for e in range(E)]
+        h = [held.tile([P, GROUP, 4], BF16, name=f"h{g}", align_bytes=64) for g in range(GROUPS)]
+        h_words = [held.tile([P, GROUP], U32, name=f"h_words{g}", align_bytes=64) for g in range(GROUPS)]
+        h_scales = [held.tile([P, GROUP], U8, name=f"h_scales{g}", align_bytes=64) for g in range(GROUPS)]
+        y_sb = [held.tile([P, GROUP], F32, name=f"y_sb{g}", align_bytes=64) for g in range(GROUPS)]
 
         def first_layer(e):
-            g, half = divmod(e, 2)
             slots = slice(e * C, (e + 1) * C)
-            v[e] = psum_v.tile([C, H], F32, name="v")
+            a = [first <= e < last for first, last in SCALE_GROUPS].index(True)
             for s in range(PASSES):
-                at = (half * PASSES + s) * 2 * H
-                sc = (e * PASSES + s) * H
+                sc = ((e - SCALE_GROUPS[a][0]) * PASSES + s) * H
                 nc.tensor.matmul_mx(
-                    out=v[e][:],
+                    out=banks[v_bank[e]][:],
                     lhsT=words[s][:, slots].bitcast(FP8X4),
                     lhsT_scale=scales[s][:, slots],
-                    rhs=w1w[g][:, at : at + 2 * H].bitcast(FP4X4),
-                    rhs_scale=w1s[:, sc : sc + H],
+                    rhs=w1w[e][:, s * 2 * H : (s + 1) * 2 * H].bitcast(FP4X4),
+                    rhs_scale=w1s[a][:, sc : sc + H],
                     start=(s == 0),
                     stop=(s == PASSES - 1),
                 )
 
         def relu(e):
-            r[e] = held.tile([C, 4, P], F32, name=f"r{e}")
-            nc.scalar.activation(out=r[e][:], in_=v[e][:].rearrange("c (p t) -> c t p", t=4), func=ACT.Relu)
+            nc.scalar.activation(out=r[e][:], in_=banks[v_bank[e]][:].rearrange("c (p t) -> c t p", t=4), func=ACT.Relu)
 
         def turn(e):
-            turned[e] = psum_t.tile([P, 4, C], F32, name="turned")
             for t in range(4):
-                nc.tensor.transpose(turned[e][:, t, :], r[e][:, t, :], ident[:])
+                nc.tensor.transpose(banks[turned_bank[e]][:, t * C : (t + 1) * C], r[e][:, t, :], ident[:])
 
         def square(e):
-            h[e] = held.tile([P, C, 4], BF16, name=f"h{e}", align_bytes=64)
-            nc.scalar.activation(out=h[e][:], in_=turned[e][:].rearrange("p t c -> p c t"), func=ACT.Square)
-
-        def quantise(e):
-            h_words[e] = held.tile([P, C], U32, name=f"h_words{e}", align_bytes=64)
-            h_scales[e] = held.tile([P, C], U8, name=f"h_scales{e}", align_bytes=64)
-            nc.vector.quantize_mx(out=h_words[e][:].bitcast(FP8X4), scales=h_scales[e][:], in_=h[e][:].rearrange("p c t -> p (c t)"))
-
-        def second_layer(e):
-            g, half = divmod(e, 2)
-            if half == 0:
-                y[g] = psum_y.tile([N, 2 * C], F32, name="y")
-            nc.tensor.matmul_mx(
-                out=y[g][:, half * C : (half + 1) * C],
-                lhsT=w2w[:, e * 2 * N : (e + 1) * 2 * N].bitcast(FP4X4),
-                lhsT_scale=w2s[:, e * N : (e + 1) * N],
-                rhs=h_words[e][:].bitcast(FP8X4),
-                rhs_scale=h_scales[e][:],
-                start=True,
-                stop=True,
+            g, side = divmod(e, 2)
+            nc.scalar.activation(
+                out=h[g][:, side * C : (side + 1) * C, :],
+                in_=banks[turned_bank[e]][:].rearrange("p (t c) -> p c t", t=4),
+                func=ACT.Square,
             )
 
-        def put_back(g):
-            cols = slice(g * GROUP, (g + 1) * GROUP)
-            nc.scalar.copy(y_sb[:, cols], y[g][:])
-            picked = offsets[:, g * GROUP // 16 : (g + 1) * GROUP // 16]
-            nc.vector.tensor_tensor(out_sb[:].indirect(picked), y_sb[:, cols], gate_sb[:, cols], MULT)
+        def quantise(g):
+            nc.vector.quantize_mx(out=h_words[g][:].bitcast(FP8X4), scales=h_scales[g][:], in_=h[g][:].rearrange("p c t -> p (c t)"))
 
-        for k in range(E + 3):
-            if k < E:
-                first_layer(k)
-                relu(k)
-            if 0 <= k - 1 < E:
-                turn(k - 1)
-                square(k - 1)
-            if 0 <= k - 2 < E:
-                quantise(k - 2)
-            if 0 <= k - 3 < E:
-                second_layer(k - 3)
-                if k % 2 == 0:
-                    put_back((k - 3) // 2)
+        def second_layer(g):
+            for side in range(2):
+                e = 2 * g + side
+                cols = slice(side * C, (side + 1) * C)
+                nc.tensor.matmul_mx(
+                    out=banks[y_bank[g]][:, cols],
+                    lhsT=w2w[e // half][:, e % half * 2 * N : (e % half + 1) * 2 * N].bitcast(FP4X4),
+                    lhsT_scale=w2s[:, e * N : (e + 1) * N],
+                    rhs=h_words[g][:, cols].bitcast(FP8X4),
+                    rhs_scale=h_scales[g][:, cols],
+                    start=True,
+                    stop=True,
+                )
+
+        def put_back(g):
+            nc.scalar.copy(y_sb[g][:], banks[y_bank[g]][:, :GROUP])
+            picked = offsets[:, g * GROUP // 16 : (g + 1) * GROUP // 16]
+            nc.vector.tensor_tensor(out_sb[:].indirect(picked), y_sb[g][:], gate_sb[:, g * GROUP : (g + 1) * GROUP], MULT)
+
+        first_layer(0)
+        first_layer(1)
+        relu(0)
+        turn(0)
+        first_layer(2)
+        relu(1)
+        turn(1)
+        first_layer(3)
+        square(0)
+        for g in range(GROUPS - 1):
+            last = g == GROUPS - 2
+            relu(2 * g + 2)
+            turn(2 * g + 2)
+            if not last:
+                first_layer(2 * g + 4)
+            square(2 * g + 1)
+            quantise(g)
+            relu(2 * g + 3)
+            if last:
+                turn(2 * g + 3)
+                second_layer(g)
+                square(2 * g + 2)
+            else:
+                second_layer(g)
+                turn(2 * g + 3)
+                square(2 * g + 2)
+                put_back(g)
+                first_layer(2 * g + 5)
+        square(E - 1)
+        quantise(GROUPS - 1)
+        put_back(GROUPS - 2)
+        second_layer(GROUPS - 1)
+        put_back(GROUPS - 1)
         nc.sync.dma_start(out=out, in_=out_sb[:])

@@ -23,19 +23,17 @@ PASSES = K // 512
 GROUP = 256
 GROUPS = SLOTS // GROUP
 
-SCALE_GROUPS = ((0, 2), (2, 5), (5, 8))
-
 CHUNKS = (
-    (0, 0, 256, 96),
-    (0, 256, 512, 160),
-    (0, 768, 512, 160),
-    (0, 1280, 512, 192),
+    (0, 0, 256, 128),
+    (0, 256, 512, 224),
+    (0, 768, 512, 224),
+    (0, 1280, 512, 256),
     (0, 1792, 256, 160),
     (1, 0, 512, 0),
-    (1, 512, 512, 0),
-    (1, 1024, 512, 160),
-    (1, 1536, 256, 96),
-    (1, 1792, 256, 144),
+    (1, 512, 512, 64),
+    (1, 1024, 512, 256),
+    (1, 1536, 256, 128),
+    (1, 1792, 256, 160),
 )
 
 
@@ -49,6 +47,19 @@ def tile_moe_pln_mlp_relu2_kernel(tc, xT, w1_words, w1_scales, w2_words, w2_scal
 
         offsets = lists.tile([P, SLOTS // 16], U16, name="offsets")
 
+        half = E // 2
+        w1s = [held.tile([P, half * PASSES * H], U8, name=f"w1s{a}", align_bytes=64) for a in range(2)]
+        w2s = held.tile([P, E * N], U8, name="w2s", align_bytes=64)
+        warm = held.tile([P, 1], F32, name="warm")
+        warm_in = held.tile([P, 1], F32, name="warm_in")
+        nc.vector.memset(warm_in[:], 0.0)
+        nc.scalar.activation(out=warm[:], in_=warm_in[:], func=ACT.Square)
+        nc.gpsimd.memset(w1s[0][:].bitcast(I32), 0)
+        nc.vector.memset(w2s[:].bitcast(I32), 0)
+        nc.vector.memset(w1s[1][:].bitcast(I32), 0)
+
+        w2s_int = w2_scales.bitcast(I32).rearrange("e o (q r) b -> r q (e o) b", r=4)
+        w2s_view = w2s[:].bitcast(I32).rearrange("p (e b) -> p e b", e=E)
         raws = []
         for i, (s, t0, width, by_vector) in enumerate(CHUNKS):
             raw = held.tile([P, 4, width], F32, name=f"raw{i}", tag=f"slot{i}", align_bytes=64)
@@ -58,45 +69,40 @@ def tile_moe_pln_mlp_relu2_kernel(tc, xT, w1_words, w1_scales, w2_words, w2_scal
                 nc.sync.dma_start(offsets[:], offs)
                 gate_cols = held.tile([P, SLOTS // P], F32, name="gate_cols")
                 nc.sync.dma_start(out=gate_cols[:], in_=gate[0].rearrange("(p j) -> p j", p=P))
-
-        w1s, w1w, w2w = {}, {}, {}
-
-        def zero_w1_scales(a, engine, tag):
-            first, last = SCALE_GROUPS[a]
-            w1s[a] = held.tile([P, (last - first) * PASSES * H], U8, name=f"w1s{a}", tag=tag, align_bytes=64)
-            engine.memset(w1s[a][:].bitcast(I32), 0)
+            if i == 4:
+                for r in range(4):
+                    nc.sync.dma_start(out=w2s_view[r:P:32], in_=w2s_int[r])
 
         out_sb = held.tile([P, T], F32, name="out_sb", align_bytes=64)
         bytes_all = [held.tile([P, T], U8, name=f"bytes_all{s}", align_bytes=64) for s in range(PASSES)]
-        warm = held.tile([P, 1], F32, name="warm")
-        warm_in = held.tile([P, 1], F32, name="warm_in")
-        nc.vector.memset(warm_in[:], 0.0)
-        nc.scalar.activation(out=warm[:], in_=warm_in[:], func=ACT.Square)
-        zero_w1_scales(0, nc.gpsimd, "w1s0")
-        zero_w1_scales(1, nc.gpsimd, "w1s1")
         for s in range(PASSES):
             nc.vector.memset(bytes_all[s][:].bitcast(I32), 0)
         ident = held.tile([P, P], F32, name="ident")
         make_identity(nc, ident[:])
 
-        w1_int = w1_words.bitcast(I32).rearrange("e s p b -> e p s b")
+        w1_int = w1_words.bitcast(I32).rearrange("e s p b -> p (e s) b")
         w1s_int = w1_scales.bitcast(I32).rearrange("e s (q r) b -> r q (e s) b", r=4)
-        w2s_int = w2_scales.bitcast(I32).rearrange("e o (q r) b -> r q (e o) b", r=4)
+        w1w = {}
 
-        def load_w1(e, tag):
-            w1w[e] = held.tile([P, PASSES * 2 * H], U8, name=f"w1w{e}", tag=tag, align_bytes=64)
-            nc.sync.dma_start(out=w1w[e][:].bitcast(I32).rearrange("p (s b) -> p s b", s=PASSES), in_=w1_int[e])
+        def load_w1(first, last, tag):
+            tile = held.tile([P, (last - first) * PASSES * 2 * H], U8, name=f"w1w{first}", tag=tag, align_bytes=64)
+            nc.sync.dma_start(
+                out=tile[:].bitcast(I32).rearrange("p (s b) -> p s b", s=(last - first) * PASSES),
+                in_=w1_int[:, first * PASSES : last * PASSES, :],
+            )
+            for e in range(first, last):
+                w1w[e] = tile[:, (e - first) * PASSES * 2 * H : (e - first + 1) * PASSES * 2 * H]
 
         def load_w1_scales(a):
-            first, last = SCALE_GROUPS[a]
-            view = w1s[a][:].bitcast(I32).rearrange("p (e b) -> p e b", e=(last - first) * PASSES)
+            view = w1s[a][:].bitcast(I32).rearrange("p (e b) -> p e b", e=half * PASSES)
             for r in range(4):
-                nc.sync.dma_start(out=view[r:P:32], in_=w1s_int[r][:, first * PASSES : last * PASSES, :])
+                nc.sync.dma_start(out=view[r:P:32], in_=w1s_int[r][:, a * half * PASSES : (a + 1) * half * PASSES, :])
 
-        for a in range(2):
-            load_w1_scales(a)
-            for e in range(*SCALE_GROUPS[a]):
-                load_w1(e, f"w1w{e}")
+        load_w1_scales(0)
+        load_w1(0, 1, "w1w0")
+        load_w1(1, 2, "w1w1")
+        load_w1(2, 4, "w1w2")
+        load_w1_scales(1)
 
         words_all = [held.tile([P, T], U32, name=f"words_all{s}", align_bytes=64) for s in range(PASSES)]
         words = [held.tile([P, SLOTS], U32, name=f"words{s}", align_bytes=64) for s in range(PASSES)]
@@ -126,25 +132,13 @@ def tile_moe_pln_mlp_relu2_kernel(tc, xT, w1_words, w1_scales, w2_words, w2_scal
             if s == 0 and t0 + width == T:
                 gather(0, 0, SLOTS)
 
-        half = E // 2
-        w2_int = w2_words.bitcast(I32).rearrange("(a e) o p b -> a p (e o) b", a=2)
-
-        def load_w2(a, tag):
-            w2w[a] = held.tile([P, half * 2 * N], U8, name=f"w2w{a}", tag=tag, align_bytes=64)
-            nc.sync.dma_start(out=w2w[a][:].bitcast(I32).rearrange("p (e b) -> p e b", e=half), in_=w2_int[a])
-
-        w2s = held.tile([P, E * N], U8, name="w2s", tag="slot0", align_bytes=64)
-        nc.vector.memset(w2s[:].bitcast(I32), 0)
-        w2s_view = w2s[:].bitcast(I32).rearrange("p (e b) -> p e b", e=E)
-        for r in range(4):
-            nc.sync.dma_start(out=w2s_view[r:P:32], in_=w2s_int[r])
-        load_w2(0, "slot1")
-        zero_w1_scales(2, nc.vector, "slot2")
-        load_w1_scales(2)
-        load_w1(5, "slot3")
-        load_w1(6, "slot4")
-        load_w1(7, "slot5")
-        load_w2(1, "slot6")
+        load_w1(4, 6, "slot0")
+        w2w = held.tile([P, E * 2 * N], U8, name="w2w", tag="slot1", align_bytes=64)
+        nc.sync.dma_start(
+            out=w2w[:].bitcast(I32).rearrange("p (e b) -> p e b", e=E),
+            in_=w2_words.bitcast(I32).rearrange("e o p b -> p (e o) b"),
+        )
+        load_w1(6, 8, "slot2")
 
         gate_sb = held.tile([P, SLOTS], F32, name="gate_sb", align_bytes=64)
         for a in range(2):
@@ -173,15 +167,14 @@ def tile_moe_pln_mlp_relu2_kernel(tc, xT, w1_words, w1_scales, w2_words, w2_scal
 
         def first_layer(e):
             slots = slice(e * C, (e + 1) * C)
-            a = [first <= e < last for first, last in SCALE_GROUPS].index(True)
             for s in range(PASSES):
-                sc = ((e - SCALE_GROUPS[a][0]) * PASSES + s) * H
+                sc = (e % half * PASSES + s) * H
                 nc.tensor.matmul_mx(
                     out=banks[v_bank[e]][:],
                     lhsT=words[s][:, slots].bitcast(FP8X4),
                     lhsT_scale=scales[s][:, slots],
                     rhs=w1w[e][:, s * 2 * H : (s + 1) * 2 * H].bitcast(FP4X4),
-                    rhs_scale=w1s[a][:, sc : sc + H],
+                    rhs_scale=w1s[e // half][:, sc : sc + H],
                     start=(s == 0),
                     stop=(s == PASSES - 1),
                 )
@@ -210,7 +203,7 @@ def tile_moe_pln_mlp_relu2_kernel(tc, xT, w1_words, w1_scales, w2_words, w2_scal
                 cols = slice(side * C, (side + 1) * C)
                 nc.tensor.matmul_mx(
                     out=banks[y_bank[g]][:, cols],
-                    lhsT=w2w[e // half][:, e % half * 2 * N : (e % half + 1) * 2 * N].bitcast(FP4X4),
+                    lhsT=w2w[:, e * 2 * N : (e + 1) * 2 * N].bitcast(FP4X4),
                     lhsT_scale=w2s[:, e * N : (e + 1) * N],
                     rhs=h_words[g][:, cols].bitcast(FP8X4),
                     rhs_scale=h_scales[g][:, cols],

@@ -75,8 +75,6 @@ def tile_moe_pln_mlp_relu2_kernel(tc, xT, w1_words, w1_scales, w2_words, w2_scal
 
         out_sb = held.tile([P, T], F32, name="out_sb", align_bytes=64)
         bytes_all = [held.tile([P, T], U8, name=f"bytes_all{s}", align_bytes=64) for s in range(PASSES)]
-        for s in range(PASSES):
-            nc.vector.memset(bytes_all[s][:].bitcast(I32), 0)
         ident = held.tile([P, P], F32, name="ident")
         make_identity(nc, ident[:])
 
@@ -105,16 +103,20 @@ def tile_moe_pln_mlp_relu2_kernel(tc, xT, w1_words, w1_scales, w2_words, w2_scal
         load_w1_scales(1)
 
         words_all = [held.tile([P, T], U32, name=f"words_all{s}", align_bytes=64) for s in range(PASSES)]
-        words = [held.tile([P, SLOTS], U32, name=f"words{s}", align_bytes=64) for s in range(PASSES)]
-        scales = [held.tile([P, SLOTS], U8, name=f"scales{s}", align_bytes=64) for s in range(PASSES)]
+        words, scales = {}, {}
 
-        def gather(s, a, b):
-            picked = offsets[:, a // 16 : b // 16]
-            nc.vector.tensor_copy(words[s][:, a:b], words_all[s][:].indirect(picked))
-            nc.vector.tensor_copy(scales[s][:, a:b], bytes_all[s][:].indirect(picked))
+        def gather(s, first, last, words_tag, scales_tag):
+            picked = offsets[:, first * C // 16 : last * C // 16]
+            codes = held.tile([P, (last - first) * C], U32, name=f"words{s}_{first}", tag=words_tag, align_bytes=64)
+            nc.vector.tensor_copy(codes[:], words_all[s][:].indirect(picked))
+            plane = held.tile([P, (last - first) * C], U8, name=f"scales{s}_{first}", tag=scales_tag, align_bytes=64)
+            nc.vector.tensor_copy(plane[:], bytes_all[s][:].indirect(picked))
+            for e in range(first, last):
+                words[s, e] = codes[:, (e - first) * C : (e - first + 1) * C]
+                scales[s, e] = plane[:, (e - first) * C : (e - first + 1) * C]
 
         for i, (s, t0, width, by_vector) in enumerate(CHUNKS):
-            piece = held.tile([P, width, 4], BF16, name=f"piece{i}", align_bytes=64)
+            piece = held.tile([P, width, 4], BF16, name=f"piece{i}", tag=f"piece{i}", align_bytes=64)
             for a, b, mover in ((0, by_vector, "v"), (by_vector, width, "s")):
                 if a == b:
                     continue
@@ -130,7 +132,7 @@ def tile_moe_pln_mlp_relu2_kernel(tc, xT, w1_words, w1_scales, w2_words, w2_scal
                 in_=piece[:].rearrange("p w t -> p (w t)"),
             )
             if s == 0 and t0 + width == T:
-                gather(0, 0, SLOTS)
+                gather(0, 0, E - 2, "words0", "scales0")
 
         load_w1(4, 6, "slot0")
         w2w = held.tile([P, E * 2 * N], U8, name="w2w", tag="slot1", align_bytes=64)
@@ -153,26 +155,25 @@ def tile_moe_pln_mlp_relu2_kernel(tc, xT, w1_words, w1_scales, w2_words, w2_scal
         for a in range(0, T, 512):
             nc.vector.memset(out_sb[:, a : a + 512], 0.0)
 
-        for g in range(GROUPS):
-            gather(PASSES - 1, g * GROUP, (g + 1) * GROUP)
+        for g in range(GROUPS - 1):
+            gather(1, 2 * g, 2 * g + 2, f"words1_{g}", f"scales1_{g}")
 
         v_bank = (0, 1, 0, 1, 0, 2, 0, 4)
         turned_bank = (2, 3, 2, 3, 4, 3, 5, 3)
         y_bank = (1, 2, 4, 6)
-        r = [held.tile([C, 4, P], F32, name=f"r{e}") for e in range(E)]
-        h = [held.tile([P, GROUP, 4], BF16, name=f"h{g}", align_bytes=64) for g in range(GROUPS)]
+        r = [held.tile([C, 4, P], F32, name=f"r{e}", tag=f"r{e}", align_bytes=64) for e in range(E)]
+        h = [held.tile([P, GROUP, 4], BF16, name=f"h{g}", tag=f"h{g}", align_bytes=64) for g in range(GROUPS)]
         h_words = [held.tile([P, GROUP], U32, name=f"h_words{g}", align_bytes=64) for g in range(GROUPS)]
-        h_scales = [held.tile([P, GROUP], U8, name=f"h_scales{g}", align_bytes=64) for g in range(GROUPS)]
+        h_scales = [held.tile([P, GROUP], U8, name=f"h_scales{g}", tag=f"h_scales{g}", align_bytes=64) for g in range(GROUPS)]
         y_sb = [held.tile([P, GROUP], F32, name=f"y_sb{g}", align_bytes=64) for g in range(GROUPS)]
 
         def first_layer(e):
-            slots = slice(e * C, (e + 1) * C)
             for s in range(PASSES):
                 sc = (e % half * PASSES + s) * H
                 nc.tensor.matmul_mx(
                     out=banks[v_bank[e]][:],
-                    lhsT=words[s][:, slots].bitcast(FP8X4),
-                    lhsT_scale=scales[s][:, slots],
+                    lhsT=words[s, e].bitcast(FP8X4),
+                    lhsT_scale=scales[s, e],
                     rhs=w1w[e][:, s * 2 * H : (s + 1) * 2 * H].bitcast(FP4X4),
                     rhs_scale=w1s[e // half][:, sc : sc + H],
                     start=(s == 0),
@@ -220,6 +221,7 @@ def tile_moe_pln_mlp_relu2_kernel(tc, xT, w1_words, w1_scales, w2_words, w2_scal
         first_layer(1)
         relu(0)
         turn(0)
+        gather(0, E - 2, E, f"piece{len(CHUNKS) - 1}", "r0")
         first_layer(2)
         relu(1)
         turn(1)
@@ -240,6 +242,8 @@ def tile_moe_pln_mlp_relu2_kernel(tc, xT, w1_words, w1_scales, w2_words, w2_scal
                 square(2 * g + 2)
             else:
                 second_layer(g)
+                if g == 0:
+                    gather(1, E - 2, E, "h0", "h_scales0")
                 turn(2 * g + 3)
                 square(2 * g + 2)
                 put_back(g)

@@ -24,16 +24,17 @@ GROUP = 256
 GROUPS = SLOTS // GROUP
 
 CHUNKS = (
-    (0, 0, 256, 128),
-    (0, 256, 512, 224),
-    (0, 768, 512, 224),
-    (0, 1280, 512, 256),
-    (0, 1792, 256, 160),
-    (1, 0, 512, 0),
-    (1, 512, 512, 64),
-    (1, 1024, 512, 256),
-    (1, 1536, 256, 128),
-    (1, 1792, 256, 160),
+    (0, 0, 1024, 640),
+    (0, 1024, 1024, 640),
+    (1, 0, 1024, 0),
+    (1, 1024, 1024, 640),
+    (2, 0, 1024, 0),
+    (2, 1024, 1024, 640),
+    (3, 0, 512, 0),
+    (3, 512, 512, 0),
+    (3, 1024, 512, 192),
+    (3, 1536, 256, 256),
+    (3, 1792, 256, 160),
 )
 
 
@@ -43,159 +44,212 @@ def tile_moe_pln_mlp_relu2_kernel(tc, xT, w1_words, w1_scales, w2_words, w2_scal
         lists = ctx.enter_context(tc.tile_pool(name="lists", bufs=1))
         held = ctx.enter_context(tc.tile_pool(name="held", bufs=1))
         psum = ctx.enter_context(tc.psum_pool(name="psum", bufs=1))
-        banks = [psum.tile([P, 512], F32, name=f"bank{b}") for b in range(7)]
+        banks = [psum.tile([P, 512], F32, name=f"bank{b}") for b in range(8)]
 
         offsets = lists.tile([P, SLOTS // 16], U16, name="offsets")
 
-        half = E // 2
-        w1s = [held.tile([P, half * PASSES * H], U8, name=f"w1s{a}", align_bytes=64) for a in range(2)]
+        runs = ((0, 2), (2, 8))
+        w1s = [held.tile([P, (last - first) * PASSES * H], U8, name=f"w1s{first}", align_bytes=64) for first, last in runs]
+        w1_scale = {e: tile[:, (e - first) * PASSES * H : (e - first + 1) * PASSES * H] for tile, (first, last) in zip(w1s, runs) for e in range(first, last)}
         w2s = held.tile([P, E * N], U8, name="w2s", align_bytes=64)
-        warm = held.tile([P, 1], F32, name="warm")
-        warm_in = held.tile([P, 1], F32, name="warm_in")
-        nc.vector.memset(warm_in[:], 0.0)
-        nc.scalar.activation(out=warm[:], in_=warm_in[:], func=ACT.Square)
-        nc.gpsimd.memset(w1s[0][:].bitcast(I32), 0)
+        nc.vector.memset(w1s[0][:].bitcast(I32), 0)
+        zeroed = w1s[1][:].bitcast(I32)
+        nc.vector.memset(zeroed[:, :512], 0)
+        nc.gpsimd.memset(zeroed[:, 512:], 0)
         nc.vector.memset(w2s[:].bitcast(I32), 0)
-        nc.vector.memset(w1s[1][:].bitcast(I32), 0)
 
-        w2s_int = w2_scales.bitcast(I32).rearrange("e o (q r) b -> r q (e o) b", r=4)
-        w2s_view = w2s[:].bitcast(I32).rearrange("p (e b) -> p e b", e=E)
+        x_rows = xT.rearrange("(s p j) t -> s p j t", s=PASSES, j=4)
         raws = []
-        for i, (s, t0, width, by_vector) in enumerate(CHUNKS):
-            raw = held.tile([P, 4, width], F32, name=f"raw{i}", tag=f"slot{i}", align_bytes=64)
-            nc.sync.dma_start(out=raw[:], in_=xT[512 * s : 512 * (s + 1), t0 : t0 + width].rearrange("(p j) w -> p j w", j=4))
+        for i, (u, t0, width, by_vector) in enumerate(CHUNKS):
+            s, v = divmod(u, 2)
+            raw = held.tile([P, 2, width], F32, name=f"raw{i}", tag=f"raw{i}", align_bytes=64)
+            nc.sync.dma_start(out=raw[:], in_=x_rows[s][:, 2 * v : 2 * v + 2, t0 : t0 + width])
             raws.append(raw)
             if i == 0:
-                nc.sync.dma_start(offsets[:], offs)
                 gate_cols = held.tile([P, SLOTS // P], F32, name="gate_cols")
                 nc.sync.dma_start(out=gate_cols[:], in_=gate[0].rearrange("(p j) -> p j", p=P))
-            if i == 4:
-                for r in range(4):
-                    nc.sync.dma_start(out=w2s_view[r:P:32], in_=w2s_int[r])
+                nc.sync.dma_start(offsets[:], offs)
 
-        out_sb = held.tile([P, T], F32, name="out_sb", align_bytes=64)
-        bytes_all = [held.tile([P, T], U8, name=f"bytes_all{s}", align_bytes=64) for s in range(PASSES)]
         ident = held.tile([P, P], F32, name="ident")
         make_identity(nc, ident[:])
+        w2s_int = w2_scales.bitcast(I32).rearrange("e o (q r) b -> r q (e o) b", r=4)
+        w2s_view = w2s[:].bitcast(I32).rearrange("p (e b) -> p e b", e=E)
 
-        w1_int = w1_words.bitcast(I32).rearrange("e s p b -> p (e s) b")
+        w1_both = w1_words.bitcast(I32).rearrange("e s p b -> p (e s) b")
         w1s_int = w1_scales.bitcast(I32).rearrange("e s (q r) b -> r q (e s) b", r=4)
-        w1w = {}
+        w2_int = w2_words.bitcast(I32).rearrange("e o p b -> p (e o) b")
+        w1w, w2w = {}, {}
 
-        def load_w1(first, last, tag):
-            tile = held.tile([P, (last - first) * PASSES * 2 * H], U8, name=f"w1w{first}", tag=tag, align_bytes=64)
-            nc.sync.dma_start(
-                out=tile[:].bitcast(I32).rearrange("p (s b) -> p s b", s=(last - first) * PASSES),
-                in_=w1_int[:, first * PASSES : last * PASSES, :],
-            )
-            for e in range(first, last):
-                w1w[e] = tile[:, (e - first) * PASSES * 2 * H : (e - first + 1) * PASSES * 2 * H]
-
-        def load_w1_scales(a):
-            view = w1s[a][:].bitcast(I32).rearrange("p (e b) -> p e b", e=half * PASSES)
+        def load_w1_scales(g):
+            first, last = runs[g]
+            view = w1s[g][:].bitcast(I32).rearrange("p (e b) -> p e b", e=(last - first) * PASSES)
             for r in range(4):
-                nc.sync.dma_start(out=view[r:P:32], in_=w1s_int[r][:, a * half * PASSES : (a + 1) * half * PASSES, :])
+                nc.sync.dma_start(out=view[r:P:32], in_=w1s_int[r][:, first * PASSES : last * PASSES, :])
+
+        def load_w1(first, last):
+            count = (last - first) * PASSES
+            tile = held.tile([P, count * 2 * H], U8, name=f"w1e{first}", tag=f"w1e{first}", align_bytes=64)
+            nc.sync.dma_start(out=tile[:].bitcast(I32).rearrange("p (s b) -> p s b", s=count), in_=w1_both[:, PASSES * first : PASSES * last, :])
+            for a in range(count):
+                w1w[first + a // PASSES, a % PASSES] = tile[:, a * 2 * H : (a + 1) * 2 * H]
+
+        def load_w2(first, last):
+            tile = held.tile([P, (last - first) * 2 * N], U8, name=f"w2w{first}", align_bytes=64)
+            nc.sync.dma_start(out=tile[:].bitcast(I32).rearrange("p (e b) -> p e b", e=last - first), in_=w2_int[:, first:last, :])
+            for e in range(first, last):
+                w2w[e] = tile[:, (e - first) * 2 * N : (e - first + 1) * 2 * N]
 
         load_w1_scales(0)
-        load_w1(0, 1, "w1w0")
-        load_w1(1, 2, "w1w1")
-        load_w1(2, 4, "w1w2")
+        load_w1(0, 1)
+        load_w1(1, 2)
         load_w1_scales(1)
+        load_w1(2, 3)
+        load_w1(3, 4)
+        load_w1(4, 5)
+        load_w1(5, 6)
+        for r in range(4):
+            nc.sync.dma_start(out=w2s_view[r:P:32], in_=w2s_int[r])
+        load_w2(0, 4)
+        load_w1(6, 7)
+        load_w1(7, 8)
+        load_w2(4, 8)
 
-        words_all = [held.tile([P, T], U32, name=f"words_all{s}", align_bytes=64) for s in range(PASSES)]
-        words, scales = {}, {}
-
-        def gather(s, first, last, words_tag, scales_tag):
-            picked = offsets[:, first * C // 16 : last * C // 16]
-            codes = held.tile([P, (last - first) * C], U32, name=f"words{s}_{first}", tag=words_tag, align_bytes=64)
-            nc.vector.tensor_copy(codes[:], words_all[s][:].indirect(picked))
-            plane = held.tile([P, (last - first) * C], U8, name=f"scales{s}_{first}", tag=scales_tag, align_bytes=64)
-            nc.vector.tensor_copy(plane[:], bytes_all[s][:].indirect(picked))
-            for e in range(first, last):
-                words[s, e] = codes[:, (e - first) * C : (e - first + 1) * C]
-                scales[s, e] = plane[:, (e - first) * C : (e - first + 1) * C]
-
-        for i, (s, t0, width, by_vector) in enumerate(CHUNKS):
-            piece = held.tile([P, width, 4], BF16, name=f"piece{i}", tag=f"piece{i}", align_bytes=64)
-            for a, b, mover in ((0, by_vector, "v"), (by_vector, width, "s")):
-                if a == b:
-                    continue
-                dst = piece[:, a:b, :].rearrange("p (c i) t -> p c t i", i=4)
-                src = raws[i][:, :, a:b].rearrange("p t (c i) -> p c t i", i=4)
-                if mover == "v":
-                    nc.vector.tensor_copy(dst, src)
-                else:
-                    nc.scalar.activation(out=dst, in_=src, func=ACT.Copy)
-            nc.vector.quantize_mx(
-                out=words_all[s][:, t0 : t0 + width].bitcast(FP8X4),
-                scales=bytes_all[s][:, t0 : t0 + width],
-                in_=piece[:].rearrange("p w t -> p (w t)"),
-            )
-            if s == 0 and t0 + width == T:
-                gather(0, 0, E - 2, "words0", "scales0")
-
-        load_w1(4, 6, "slot0")
-        w2w = held.tile([P, E * 2 * N], U8, name="w2w", tag="slot1", align_bytes=64)
-        nc.sync.dma_start(
-            out=w2w[:].bitcast(I32).rearrange("p (e b) -> p e b", e=E),
-            in_=w2_words.bitcast(I32).rearrange("e o p b -> p (e o) b"),
-        )
-        load_w1(6, 8, "slot2")
+        out_sb = held.tile([P, T], F32, name="out_sb", align_bytes=64)
+        for a in range(0, T, 1024):
+            nc.vector.memset(out_sb[:, a : a + 1024], 0.0)
 
         gate_sb = held.tile([P, SLOTS], F32, name="gate_sb", align_bytes=64)
         for a in range(2):
             for j in range(4):
                 column = gate_cols[:, 4 * a + j : 4 * a + j + 1].to_broadcast([P, P])
-                nc.tensor.transpose(banks[a][:, j * P : (j + 1) * P], column, ident[:])
-            nc.scalar.copy(
+                nc.tensor.transpose(banks[6 + a][:, j * P : (j + 1) * P], column, ident[:])
+            nc.vector.tensor_copy(
                 gate_sb[:].rearrange("q (p a j) -> q a p j", a=2, j=4)[:, a],
-                banks[a][:].rearrange("q (j p) -> q p j", j=4),
+                banks[6 + a][:].rearrange("q (j p) -> q p j", j=4),
             )
 
-        for a in range(0, T, 512):
-            nc.vector.memset(out_sb[:, a : a + 512], 0.0)
+        pairs = [held.tile([P, 2 * T], BF16, name=f"pairs{u}", align_bytes=64) for u in range(2 * PASSES)]
+        front = held.tile([P, 4 * 2 * GROUP], BF16, name="front", align_bytes=64)
+        planes = held.tile([P, 2 * 2 * GROUP], U32, name="planes", align_bytes=64)
+        late = held.tile([P, 4 * GROUP], U32, name="late", align_bytes=64)
+        woven1 = {g: held.tile([P, 4 * GROUP], BF16, name=f"woven1_{g}", align_bytes=64)[:] for g in range(2)}
+        third = {1: 2, 2: 1, 3: 0}
+        fourth = {1: 3, 2: 3, 3: 2}
+        words, scales, woven = {}, {}, {}
 
-        for g in range(GROUPS - 1):
-            gather(1, 2 * g, 2 * g + 2, f"words1_{g}", f"scales1_{g}")
+        def block(b):
+            return late[:, b * GROUP : (b + 1) * GROUP]
 
-        v_bank = (0, 1, 0, 1, 0, 2, 0, 4)
-        turned_bank = (2, 3, 2, 3, 4, 3, 5, 3)
-        y_bank = (1, 2, 4, 6)
-        r = [held.tile([C, 4, P], F32, name=f"r{e}", tag=f"r{e}", align_bytes=64) for e in range(E)]
-        h = [held.tile([P, GROUP, 4], BF16, name=f"h{g}", tag=f"h{g}", align_bytes=64) for g in range(GROUPS)]
-        h_words = [held.tile([P, GROUP], U32, name=f"h_words{g}", align_bytes=64) for g in range(GROUPS)]
-        h_scales = [held.tile([P, GROUP], U8, name=f"h_scales{g}", tag=f"h_scales{g}", align_bytes=64) for g in range(GROUPS)]
-        y_sb = [held.tile([P, GROUP], F32, name=f"y_sb{g}", align_bytes=64) for g in range(GROUPS)]
+        def by_pair(ap, dtype):
+            return ap.bitcast(dtype).rearrange("p (c u) -> p c u", u=2)
 
-        def first_layer(e):
-            for s in range(PASSES):
-                sc = (e % half * PASSES + s) * H
-                nc.tensor.matmul_mx(
-                    out=banks[v_bank[e]][:],
-                    lhsT=words[s, e].bitcast(FP8X4),
-                    lhsT_scale=scales[s, e],
-                    rhs=w1w[e][:, s * 2 * H : (s + 1) * 2 * H].bitcast(FP4X4),
-                    rhs_scale=w1s[e // half][:, sc : sc + H],
-                    start=(s == 0),
-                    stop=(s == PASSES - 1),
-                )
+        def gather(dst, u, first, count):
+            nc.vector.tensor_copy(dst, pairs[u][:].bitcast(U32).indirect(offsets[:, first // 16 : (first + count) // 16]))
+
+        def weave_first(g, tag):
+            woven[g] = held.tile([P, PASSES * 4 * GROUP], BF16, name=f"woven_{g}", tag=tag, align_bytes=64)
+            woven1[g] = woven[g][:, 4 * GROUP :]
+            src = planes[:].rearrange("p (u c) -> p c u", u=2)[:, (g - 2) * GROUP : (g - 1) * GROUP, :]
+            nc.scalar.copy(by_pair(woven[g][:, : 4 * GROUP], U32), src)
+
+        def weave_second(g):
+            picked = slice(third[g], fourth[g] + 1, fourth[g] - third[g])
+            if g == 1:
+                nc.scalar.copy(by_pair(woven1[g], U32), late[:].rearrange("p (b c) -> p b c", b=4)[:, picked, :].rearrange("p u c -> p c u"))
+            else:
+                nc.vector.tensor_copy(by_pair(woven1[g], I32), late[:].bitcast(I32).rearrange("p (b c) -> p b c", b=4)[:, picked, :].rearrange("p u c -> p c u"))
+
+        def quantise_x(keys, src, tag):
+            count = C * len(keys)
+            codes = held.tile([P, count], U32, name=f"words_{tag}", tag=tag, align_bytes=64)
+            plane = held.tile([P, count], U8, name=f"scales_{tag}", align_bytes=64)
+            nc.vector.quantize_mx(out=codes[:].bitcast(FP8X4), scales=plane[:], in_=src)
+            for a, key in enumerate(keys):
+                words[key] = codes[:, a * C : (a + 1) * C]
+                scales[key] = plane[:, a * C : (a + 1) * C]
+
+        def quantise_group(g, tag):
+            quantise_x([(s, e) for s in range(PASSES) for e in (2 * g, 2 * g + 1)], woven[g][:], tag)
+
+        for i, (u, t0, width, by_vector) in enumerate(CHUNKS):
+            for a, b, mover in ((0, by_vector, "v"), (by_vector, width, "s")):
+                if a == b:
+                    continue
+                dst = pairs[u][:, 2 * (t0 + a) : 2 * (t0 + b)].rearrange("p (c i j) -> p c j i", i=4, j=2)
+                src = raws[i][:, :, a:b].rearrange("p j (c i) -> p c j i", i=4)
+                if mover == "v":
+                    nc.vector.tensor_copy(dst, src)
+                else:
+                    nc.scalar.activation(out=dst, in_=src, func=ACT.Copy)
+            if t0 + width < T:
+                continue
+            if u < 2:
+                gather(by_pair(front[:], U32)[:, :, u], u, 0, 2 * GROUP)
+                gather(planes[:, u * 2 * GROUP : (u + 1) * 2 * GROUP], u, 2 * GROUP, 2 * GROUP)
+            if u == 1:
+                quantise_x([(0, e) for e in range(4)], front[:], "front_codes")
+            if u == 2:
+                gather(by_pair(woven1[0], U32)[:, :, 0], u, 0, GROUP)
+                for g in range(1, GROUPS):
+                    gather(block(third[g]), u, g * GROUP, GROUP)
+
+        for g in range(2, GROUPS):
+            weave_first(g, f"raw{len(CHUNKS) - 4 + g}")
+        gather(by_pair(woven1[0], U32)[:, :, 1], 3, 0, GROUP)
+        gather(block(fourth[1]), 3, GROUP, GROUP)
+        quantise_x([(1, 0), (1, 1)], woven1[0], "first")
+        weave_second(1)
+        quantise_x([(1, 2), (1, 3)], woven1[1], "second")
+        for g in range(2, GROUPS):
+            gather(block(fourth[g]), 3, g * GROUP, GROUP)
+        for g in range(2, GROUPS):
+            weave_second(g)
+        quantise_group(2, "group2")
+
+        r = {}
+        h, h_words = {}, {}
+        h_scales = [held.tile([P, GROUP], U8, name=f"h_scales{g}", align_bytes=64) for g in range(GROUPS)]
+
+        def v_bank(e):
+            return banks[e % 3]
+
+        def turned_bank(e):
+            return banks[3 + e % 3]
+
+        def y_bank(g):
+            return turned_bank(E - 2) if g == GROUPS - 2 else banks[6 + g % 2]
+
+        def first_layer(e, s):
+            nc.tensor.matmul_mx(
+                out=v_bank(e)[:],
+                lhsT=words[s, e].bitcast(FP8X4),
+                lhsT_scale=scales[s, e],
+                rhs=w1w[e, s].bitcast(FP4X4),
+                rhs_scale=w1_scale[e][:, s * H : (s + 1) * H],
+                start=(s == 0),
+                stop=(s == PASSES - 1),
+            )
 
         def relu(e):
-            nc.scalar.activation(out=r[e][:], in_=banks[v_bank[e]][:].rearrange("c (p t) -> c t p", t=4), func=ACT.Relu)
+            r[e] = held.tile([C, 4, P], F32, name=f"r{e}", tag=f"r{e}", align_bytes=64)
+            nc.scalar.activation(out=r[e][:], in_=v_bank(e)[:].rearrange("c (p t) -> c t p", t=4), func=ACT.Relu)
 
         def turn(e):
             for t in range(4):
-                nc.tensor.transpose(banks[turned_bank[e]][:, t * C : (t + 1) * C], r[e][:, t, :], ident[:])
+                nc.tensor.transpose(turned_bank(e)[:, t * C : (t + 1) * C], r[e][:, t, :], ident[:])
 
         def square(e):
             g, side = divmod(e, 2)
+            if side == 0:
+                h[g] = held.tile([P, GROUP, 4], BF16, name=f"h{g}", tag=f"hidden{g}", align_bytes=64)
             nc.scalar.activation(
                 out=h[g][:, side * C : (side + 1) * C, :],
-                in_=banks[turned_bank[e]][:].rearrange("p (t c) -> p c t", t=4),
+                in_=turned_bank(e)[:].rearrange("p (t c) -> p c t", t=4),
                 func=ACT.Square,
             )
 
-        def quantise(g):
+        def quantise_h(g):
+            h_words[g] = held.tile([P, GROUP], U32, name=f"h_words{g}", tag=(f"h_words{g}" if g else "w1e2"), align_bytes=64)
             nc.vector.quantize_mx(out=h_words[g][:].bitcast(FP8X4), scales=h_scales[g][:], in_=h[g][:].rearrange("p c t -> p (c t)"))
 
         def second_layer(g):
@@ -203,8 +257,8 @@ def tile_moe_pln_mlp_relu2_kernel(tc, xT, w1_words, w1_scales, w2_words, w2_scal
                 e = 2 * g + side
                 cols = slice(side * C, (side + 1) * C)
                 nc.tensor.matmul_mx(
-                    out=banks[y_bank[g]][:, cols],
-                    lhsT=w2w[:, e * 2 * N : (e + 1) * 2 * N].bitcast(FP4X4),
+                    out=y_bank(g)[:, cols],
+                    lhsT=w2w[e].bitcast(FP4X4),
                     lhsT_scale=w2s[:, e * N : (e + 1) * N],
                     rhs=h_words[g][:, cols].bitcast(FP8X4),
                     rhs_scale=h_scales[g][:, cols],
@@ -213,44 +267,47 @@ def tile_moe_pln_mlp_relu2_kernel(tc, xT, w1_words, w1_scales, w2_words, w2_scal
                 )
 
         def put_back(g):
-            nc.scalar.copy(y_sb[g][:], banks[y_bank[g]][:, :GROUP])
+            y_sb = held.tile([P, GROUP], F32, name=f"y_sb{g}", align_bytes=64)
+            nc.scalar.copy(y_sb[:], y_bank(g)[:, :GROUP])
             picked = offsets[:, g * GROUP // 16 : (g + 1) * GROUP // 16]
-            nc.vector.tensor_tensor(out_sb[:].indirect(picked), y_sb[g][:], gate_sb[:, g * GROUP : (g + 1) * GROUP], MULT)
+            nc.vector.tensor_tensor(out_sb[:].indirect(picked), y_sb[:], gate_sb[:, g * GROUP : (g + 1) * GROUP], MULT)
 
-        first_layer(0)
-        first_layer(1)
-        relu(0)
-        turn(0)
-        gather(0, E - 2, E, f"piece{len(CHUNKS) - 1}", "r0")
-        first_layer(2)
-        relu(1)
-        turn(1)
-        first_layer(3)
+        def both_passes(e):
+            for s in range(PASSES):
+                first_layer(e, s)
+
+        both_passes(0)
+        both_passes(1)
+
+        def step(e):
+            relu(e)
+            turn(e)
+            if e + 3 < E:
+                both_passes(e + 3)
+
+        both_passes(2)
+        step(0)
+        step(1)
         square(0)
-        for g in range(GROUPS - 1):
-            last = g == GROUPS - 2
-            relu(2 * g + 2)
-            turn(2 * g + 2)
-            if not last:
-                first_layer(2 * g + 4)
-            square(2 * g + 1)
-            quantise(g)
-            relu(2 * g + 3)
-            if last:
-                turn(2 * g + 3)
-                second_layer(g)
-                square(2 * g + 2)
-            else:
-                second_layer(g)
-                if g == 0:
-                    gather(1, E - 2, E, "h0", "h_scales0")
-                turn(2 * g + 3)
-                square(2 * g + 2)
-                put_back(g)
-                first_layer(2 * g + 5)
-        square(E - 1)
-        quantise(GROUPS - 1)
-        put_back(GROUPS - 2)
-        second_layer(GROUPS - 1)
+        square(1)
+        quantise_h(0)
+        quantise_group(GROUPS - 1, "hidden0")
+        second_layer(0)
+        step(2)
+        step(3)
+        for e in range(2, E):
+            if e + 2 < E:
+                step(e + 2)
+            square(e)
+            if e == 2:
+                put_back(0)
+            if e == E - 2:
+                second_layer(GROUPS - 2)
+            if e % 2:
+                quantise_h(e // 2)
+                if e != E - 3:
+                    second_layer(e // 2)
+                if e > 3:
+                    put_back(e // 2 - 1)
         put_back(GROUPS - 1)
         nc.sync.dma_start(out=out, in_=out_sb[:])

@@ -20,7 +20,7 @@ MULT = mybir.AluOpType.mult
 
 P = 128
 PASSES = K // 512
-GROUP = 256
+GROUP = 2 * C
 GROUPS = SLOTS // GROUP
 
 CHUNKS = (
@@ -30,12 +30,21 @@ CHUNKS = (
     (1, 1024, 1024, 640),
     (2, 0, 1024, 0),
     (2, 1024, 1024, 640),
-    (3, 0, 512, 0),
-    (3, 512, 512, 0),
-    (3, 1024, 512, 192),
-    (3, 1536, 256, 256),
-    (3, 1792, 256, 160),
+    (3, 0, 1024, 0),
+    (3, 1024, 512, 512),
+    (3, 1536, 512, 320),
 )
+
+SCALE_RUNS = ((0, 2), (2, E))
+
+THIRD_PAIR_BLOCK = {1: 2, 2: 1, 3: 0}
+LAST_PAIR_BLOCK = {1: 3, 2: 4, 3: 2}
+
+SUM_BANK = (0, 1, 2, 3, 0, 1, 1, 5)
+TURNED_BANK = (4, 5, 4, 5, 2, 3, 4, 0)
+SPARE_BANK = 6
+
+RELU_ON_VECTOR = 6
 
 
 def tile_moe_pln_mlp_relu2_kernel(tc, xT, w1_words, w1_scales, w2_words, w2_scales, gate, offs, out):
@@ -48,17 +57,21 @@ def tile_moe_pln_mlp_relu2_kernel(tc, xT, w1_words, w1_scales, w2_words, w2_scal
 
         offsets = lists.tile([P, SLOTS // 16], U16, name="offsets")
 
-        runs = ((0, 2), (2, 8))
-        w1s = [held.tile([P, (last - first) * PASSES * H], U8, name=f"w1s{first}", align_bytes=64) for first, last in runs]
-        w1_scale = {e: tile[:, (e - first) * PASSES * H : (e - first + 1) * PASSES * H] for tile, (first, last) in zip(w1s, runs) for e in range(first, last)}
-        w2s = held.tile([P, E * N], U8, name="w2s", align_bytes=64)
-        nc.vector.memset(w1s[0][:].bitcast(I32), 0)
-        zeroed = w1s[1][:].bitcast(I32)
-        nc.vector.memset(zeroed[:, :512], 0)
-        nc.gpsimd.memset(zeroed[:, 512:], 0)
-        nc.vector.memset(w2s[:].bitcast(I32), 0)
+        w1_scale_tiles = [held.tile([P, (last - first) * PASSES * H], U8, name=f"w1s{first}", align_bytes=64) for first, last in SCALE_RUNS]
+        w1_scale = {
+            e: tile[:, (e - first) * PASSES * H : (e - first + 1) * PASSES * H]
+            for tile, (first, last) in zip(w1_scale_tiles, SCALE_RUNS)
+            for e in range(first, last)
+        }
+        w2_scale = held.tile([P, E * N], U8, name="w2s", align_bytes=64)
+        nc.vector.memset(w1_scale_tiles[0][:].bitcast(I32), 0)
+        long_run = w1_scale_tiles[1][:].bitcast(I32)
+        a_third = long_run.shape[1] // 3
+        nc.vector.memset(long_run[:, :a_third], 0)
+        nc.gpsimd.memset(long_run[:, a_third:], 0)
+        nc.vector.memset(w2_scale[:].bitcast(I32), 0)
 
-        x_rows = xT.rearrange("(s p j) t -> s p j t", s=PASSES, j=4)
+        x_rows = xT.rearrange("(s p t) token -> s p t token", s=PASSES, t=4)
         raws = []
         for i, (u, t0, width, by_vector) in enumerate(CHUNKS):
             s, v = divmod(u, 2)
@@ -72,185 +85,187 @@ def tile_moe_pln_mlp_relu2_kernel(tc, xT, w1_words, w1_scales, w2_words, w2_scal
 
         ident = held.tile([P, P], F32, name="ident")
         make_identity(nc, ident[:])
-        w2s_int = w2_scales.bitcast(I32).rearrange("e o (q r) b -> r q (e o) b", r=4)
-        w2s_view = w2s[:].bitcast(I32).rearrange("p (e b) -> p e b", e=E)
 
-        w1_both = w1_words.bitcast(I32).rearrange("e s p b -> p (e s) b")
-        w1s_int = w1_scales.bitcast(I32).rearrange("e s (q r) b -> r q (e s) b", r=4)
-        w2_int = w2_words.bitcast(I32).rearrange("e o p b -> p (e o) b")
-        w1w, w2w = {}, {}
+        w1_words_int = w1_words.bitcast(I32).rearrange("e s p b -> p (e s) b")
+        w2_words_int = w2_words.bitcast(I32).rearrange("e o p b -> p (e o) b")
+        w1_scales_int = w1_scales.bitcast(I32).rearrange("e s (q r) b -> r q (e s) b", r=4)
+        w2_scales_int = w2_scales.bitcast(I32).rearrange("e o (q r) b -> r q (e o) b", r=4)
+        w1_code, w2_code = {}, {}
 
-        def load_w1_scales(g):
-            first, last = runs[g]
-            view = w1s[g][:].bitcast(I32).rearrange("p (e b) -> p e b", e=(last - first) * PASSES)
+        def load_w1_scales(run):
+            first, last = SCALE_RUNS[run]
+            rows = w1_scale_tiles[run][:].bitcast(I32).rearrange("p (e b) -> p e b", e=(last - first) * PASSES)
             for r in range(4):
-                nc.sync.dma_start(out=view[r:P:32], in_=w1s_int[r][:, first * PASSES : last * PASSES, :])
+                nc.sync.dma_start(out=rows[r:P:32], in_=w1_scales_int[r][:, first * PASSES : last * PASSES, :])
 
-        def load_w1(first, last):
-            count = (last - first) * PASSES
-            tile = held.tile([P, count * 2 * H], U8, name=f"w1e{first}", tag=f"w1e{first}", align_bytes=64)
-            nc.sync.dma_start(out=tile[:].bitcast(I32).rearrange("p (s b) -> p s b", s=count), in_=w1_both[:, PASSES * first : PASSES * last, :])
-            for a in range(count):
-                w1w[first + a // PASSES, a % PASSES] = tile[:, a * 2 * H : (a + 1) * 2 * H]
+        def load_w2_scales():
+            rows = w2_scale[:].bitcast(I32).rearrange("p (e b) -> p e b", e=E)
+            for r in range(4):
+                nc.sync.dma_start(out=rows[r:P:32], in_=w2_scales_int[r])
+
+        def load_w1_first_group(s):
+            tile = held.tile([P, 2 * 2 * H], U8, name=f"w1p{s}", align_bytes=64)
+            nc.sync.dma_start(out=tile[:].bitcast(I32).rearrange("p (e b) -> p e b", e=2), in_=w1_words_int[:, s : 2 * PASSES : PASSES, :])
+            for e in range(2):
+                w1_code[e, s] = tile[:, e * 2 * H : (e + 1) * 2 * H]
+
+        def load_w1(e):
+            tile = held.tile([P, PASSES * 2 * H], U8, name=f"w1e{e}", tag=f"w1e{e}", align_bytes=64)
+            nc.sync.dma_start(out=tile[:].bitcast(I32).rearrange("p (s b) -> p s b", s=PASSES), in_=w1_words_int[:, PASSES * e : PASSES * (e + 1), :])
+            for s in range(PASSES):
+                w1_code[e, s] = tile[:, s * 2 * H : (s + 1) * 2 * H]
 
         def load_w2(first, last):
             tile = held.tile([P, (last - first) * 2 * N], U8, name=f"w2w{first}", align_bytes=64)
-            nc.sync.dma_start(out=tile[:].bitcast(I32).rearrange("p (e b) -> p e b", e=last - first), in_=w2_int[:, first:last, :])
+            nc.sync.dma_start(out=tile[:].bitcast(I32).rearrange("p (e b) -> p e b", e=last - first), in_=w2_words_int[:, first:last, :])
             for e in range(first, last):
-                w2w[e] = tile[:, (e - first) * 2 * N : (e - first + 1) * 2 * N]
+                w2_code[e] = tile[:, (e - first) * 2 * N : (e - first + 1) * 2 * N]
 
         load_w1_scales(0)
-        load_w1(0, 1)
-        load_w1(1, 2)
+        for s in range(PASSES):
+            load_w1_first_group(s)
+        load_w2_scales()
+        load_w2(0, 2)
         load_w1_scales(1)
-        load_w1(2, 3)
-        load_w1(3, 4)
-        load_w1(4, 5)
-        load_w1(5, 6)
-        for r in range(4):
-            nc.sync.dma_start(out=w2s_view[r:P:32], in_=w2s_int[r])
-        load_w2(0, 4)
-        load_w1(6, 7)
-        load_w1(7, 8)
-        load_w2(4, 8)
+        for e in range(2, E):
+            load_w1(e)
+        load_w2(2, E)
 
         out_sb = held.tile([P, T], F32, name="out_sb", align_bytes=64)
-        for a in range(0, T, 1024):
-            nc.vector.memset(out_sb[:, a : a + 1024], 0.0)
+        for first in range(0, T, T // 2):
+            nc.vector.memset(out_sb[:, first : first + T // 2], 0.0)
 
         gate_sb = held.tile([P, SLOTS], F32, name="gate_sb", align_bytes=64)
-        for a in range(2):
+        for half in range(2):
+            bank = banks[SPARE_BANK + half]
             for j in range(4):
-                column = gate_cols[:, 4 * a + j : 4 * a + j + 1].to_broadcast([P, P])
-                nc.tensor.transpose(banks[6 + a][:, j * P : (j + 1) * P], column, ident[:])
+                column = gate_cols[:, 4 * half + j : 4 * half + j + 1].to_broadcast([P, P])
+                nc.tensor.transpose(bank[:, j * P : (j + 1) * P], column, ident[:])
             nc.vector.tensor_copy(
-                gate_sb[:].rearrange("q (p a j) -> q a p j", a=2, j=4)[:, a],
-                banks[6 + a][:].rearrange("q (j p) -> q p j", j=4),
+                gate_sb[:].rearrange("n (p half j) -> n half p j", half=2, j=4)[:, half],
+                bank[:].rearrange("n (j p) -> n p j", j=4),
             )
 
         pairs = [held.tile([P, 2 * T], BF16, name=f"pairs{u}", align_bytes=64) for u in range(2 * PASSES)]
-        front = held.tile([P, 4 * 2 * GROUP], BF16, name="front", align_bytes=64)
-        planes = held.tile([P, 2 * 2 * GROUP], U32, name="planes", align_bytes=64)
-        late = held.tile([P, 4 * GROUP], U32, name="late", align_bytes=64)
-        woven1 = {g: held.tile([P, 4 * GROUP], BF16, name=f"woven1_{g}", align_bytes=64)[:] for g in range(2)}
-        third = {1: 2, 2: 1, 3: 0}
-        fourth = {1: 3, 2: 3, 3: 2}
-        words, scales, woven = {}, {}, {}
+        first_pass_woven = held.tile([P, 4 * 2 * GROUP], BF16, name="front", align_bytes=64)
+        first_pass_runs = held.tile([P, 2 * 2 * GROUP], U32, name="planes", align_bytes=64)
+        blocks = held.tile([P, 5 * GROUP], U32, name="late", align_bytes=64)
+        group1_woven = held.tile([P, 4 * GROUP], BF16, name="second_woven", align_bytes=64)
+        second_pass_woven = {0: blocks[:, 3 * GROUP :].bitcast(BF16), 1: group1_woven[:]}
+        words, scales, both_woven = {}, {}, {}
 
         def block(b):
-            return late[:, b * GROUP : (b + 1) * GROUP]
+            return blocks[:, b * GROUP : (b + 1) * GROUP]
 
-        def by_pair(ap, dtype):
-            return ap.bitcast(dtype).rearrange("p (c u) -> p c u", u=2)
+        def by_pair(woven, dtype):
+            return woven.bitcast(dtype).rearrange("p (c v) -> p c v", v=2)
 
         def gather(dst, u, first, count):
             nc.vector.tensor_copy(dst, pairs[u][:].bitcast(U32).indirect(offsets[:, first // 16 : (first + count) // 16]))
 
-        def weave_first(g, tag):
-            woven[g] = held.tile([P, PASSES * 4 * GROUP], BF16, name=f"woven_{g}", tag=tag, align_bytes=64)
-            woven1[g] = woven[g][:, 4 * GROUP :]
-            src = planes[:].rearrange("p (u c) -> p c u", u=2)[:, (g - 2) * GROUP : (g - 1) * GROUP, :]
-            nc.scalar.copy(by_pair(woven[g][:, : 4 * GROUP], U32), src)
+        def weave_first_pass(g, slot):
+            both_woven[g] = held.tile([P, PASSES * 4 * GROUP], BF16, name=f"woven_{g}", tag=slot, align_bytes=64)
+            second_pass_woven[g] = both_woven[g][:, 4 * GROUP :]
+            src = first_pass_runs[:].rearrange("p (v c) -> p c v", v=2)[:, (g - 2) * GROUP : (g - 1) * GROUP, :]
+            nc.scalar.copy(by_pair(both_woven[g][:, : 4 * GROUP], U32), src)
 
-        def weave_second(g):
-            picked = slice(third[g], fourth[g] + 1, fourth[g] - third[g])
-            if g == 1:
-                nc.scalar.copy(by_pair(woven1[g], U32), late[:].rearrange("p (b c) -> p b c", b=4)[:, picked, :].rearrange("p u c -> p c u"))
-            else:
-                nc.vector.tensor_copy(by_pair(woven1[g], I32), late[:].bitcast(I32).rearrange("p (b c) -> p b c", b=4)[:, picked, :].rearrange("p u c -> p c u"))
+        def weave_second_pass(g):
+            low, high = THIRD_PAIR_BLOCK[g], LAST_PAIR_BLOCK[g]
+            src = blocks[:].bitcast(I32).rearrange("p (b c) -> p b c", c=GROUP)[:, low : high + 1 : high - low, :]
+            nc.vector.tensor_copy(by_pair(second_pass_woven[g], I32), src.rearrange("p v c -> p c v"))
 
-        def quantise_x(keys, src, tag):
+        def quantise_tokens(keys, woven, slot):
             count = C * len(keys)
-            codes = held.tile([P, count], U32, name=f"words_{tag}", tag=tag, align_bytes=64)
-            plane = held.tile([P, count], U8, name=f"scales_{tag}", align_bytes=64)
-            nc.vector.quantize_mx(out=codes[:].bitcast(FP8X4), scales=plane[:], in_=src)
+            codes = held.tile([P, count], U32, name=f"words_{slot}", tag=slot, align_bytes=64)
+            scale_bytes = held.tile([P, count], U8, name=f"scales_{slot}", align_bytes=64)
+            nc.vector.quantize_mx(out=codes[:].bitcast(FP8X4), scales=scale_bytes[:], in_=woven)
             for a, key in enumerate(keys):
                 words[key] = codes[:, a * C : (a + 1) * C]
-                scales[key] = plane[:, a * C : (a + 1) * C]
+                scales[key] = scale_bytes[:, a * C : (a + 1) * C]
 
-        def quantise_group(g, tag):
-            quantise_x([(s, e) for s in range(PASSES) for e in (2 * g, 2 * g + 1)], woven[g][:], tag)
+        def quantise_both_passes(g, slot):
+            quantise_tokens([(s, e) for s in range(PASSES) for e in (2 * g, 2 * g + 1)], both_woven[g][:], slot)
 
         for i, (u, t0, width, by_vector) in enumerate(CHUNKS):
-            for a, b, mover in ((0, by_vector, "v"), (by_vector, width, "s")):
-                if a == b:
-                    continue
-                dst = pairs[u][:, 2 * (t0 + a) : 2 * (t0 + b)].rearrange("p (c i j) -> p c j i", i=4, j=2)
-                src = raws[i][:, :, a:b].rearrange("p j (c i) -> p c j i", i=4)
-                if mover == "v":
-                    nc.vector.tensor_copy(dst, src)
-                else:
-                    nc.scalar.activation(out=dst, in_=src, func=ACT.Copy)
+            dst = pairs[u][:, 2 * t0 : 2 * (t0 + width)].rearrange("p (c i j) -> p c j i", i=4, j=2)
+            src = raws[i][:].rearrange("p j (c i) -> p c j i", i=4)
+            cut = by_vector // 4
+            if by_vector > 0:
+                nc.vector.tensor_copy(dst[:, :cut], src[:, :cut])
+            if by_vector < width:
+                nc.scalar.activation(out=dst[:, cut:], in_=src[:, cut:], func=ACT.Copy)
             if t0 + width < T:
                 continue
             if u < 2:
-                gather(by_pair(front[:], U32)[:, :, u], u, 0, 2 * GROUP)
-                gather(planes[:, u * 2 * GROUP : (u + 1) * 2 * GROUP], u, 2 * GROUP, 2 * GROUP)
+                gather(by_pair(first_pass_woven[:], U32)[:, :, u], u, 0, 2 * GROUP)
+                gather(first_pass_runs[:, u * 2 * GROUP : (u + 1) * 2 * GROUP], u, 2 * GROUP, 2 * GROUP)
             if u == 1:
-                quantise_x([(0, e) for e in range(4)], front[:], "front_codes")
+                quantise_tokens([(0, e) for e in range(4)], first_pass_woven[:], "front_codes")
             if u == 2:
-                gather(by_pair(woven1[0], U32)[:, :, 0], u, 0, GROUP)
+                gather(by_pair(second_pass_woven[0], U32)[:, :, 0], u, 0, GROUP)
                 for g in range(1, GROUPS):
-                    gather(block(third[g]), u, g * GROUP, GROUP)
+                    gather(block(THIRD_PAIR_BLOCK[g]), u, g * GROUP, GROUP)
 
+        for g, chunk in ((2, len(CHUNKS) - 2), (3, len(CHUNKS) - 1)):
+            weave_first_pass(g, f"raw{chunk}")
+
+        last = 2 * PASSES - 1
+        gather(by_pair(second_pass_woven[0], U32)[:, :, 1], last, 0, GROUP)
+        quantise_tokens([(1, 0), (1, 1)], second_pass_woven[0], "first")
+        gather(block(LAST_PAIR_BLOCK[1]), last, GROUP, GROUP)
+        weave_second_pass(1)
+        gather(block(LAST_PAIR_BLOCK[2]), last, 2 * GROUP, GROUP)
+        quantise_tokens([(1, 2), (1, 3)], second_pass_woven[1], "second")
+        gather(block(LAST_PAIR_BLOCK[3]), last, 3 * GROUP, GROUP)
         for g in range(2, GROUPS):
-            weave_first(g, f"raw{len(CHUNKS) - 4 + g}")
-        gather(by_pair(woven1[0], U32)[:, :, 1], 3, 0, GROUP)
-        gather(block(fourth[1]), 3, GROUP, GROUP)
-        quantise_x([(1, 0), (1, 1)], woven1[0], "first")
-        weave_second(1)
-        quantise_x([(1, 2), (1, 3)], woven1[1], "second")
-        for g in range(2, GROUPS):
-            gather(block(fourth[g]), 3, g * GROUP, GROUP)
-        for g in range(2, GROUPS):
-            weave_second(g)
-        quantise_group(2, "group2")
+            weave_second_pass(g)
+        quantise_both_passes(2, "group2")
 
-        r = {}
-        h, h_words = {}, {}
-        h_scales = [held.tile([P, GROUP], U8, name=f"h_scales{g}", align_bytes=64) for g in range(GROUPS)]
-
-        def v_bank(e):
-            return banks[e % 3]
-
-        def turned_bank(e):
-            return banks[3 + e % 3]
+        relued, hidden, hidden_words = {}, {}, {}
+        hidden_scales = [held.tile([P, GROUP], U8, name=f"h_scales{g}", align_bytes=64) for g in range(GROUPS)]
 
         def y_bank(g):
-            return turned_bank(E - 2) if g == GROUPS - 2 else banks[6 + g % 2]
+            return banks[TURNED_BANK[E - 2]] if g == GROUPS - 2 else banks[SPARE_BANK + g % 2]
 
-        def first_layer(e, s):
+        def first_layer_pass(e, s):
             nc.tensor.matmul_mx(
-                out=v_bank(e)[:],
+                out=banks[SUM_BANK[e]][:],
                 lhsT=words[s, e].bitcast(FP8X4),
                 lhsT_scale=scales[s, e],
-                rhs=w1w[e, s].bitcast(FP4X4),
+                rhs=w1_code[e, s].bitcast(FP4X4),
                 rhs_scale=w1_scale[e][:, s * H : (s + 1) * H],
                 start=(s == 0),
                 stop=(s == PASSES - 1),
             )
 
-        def relu(e):
-            r[e] = held.tile([C, 4, P], F32, name=f"r{e}", tag=f"r{e}", align_bytes=64)
-            nc.scalar.activation(out=r[e][:], in_=v_bank(e)[:].rearrange("c (p t) -> c t p", t=4), func=ACT.Relu)
+        def first_layer(e):
+            for s in range(PASSES):
+                first_layer_pass(e, s)
 
-        def turn(e):
+        def relu_and_turn(e):
+            relued[e] = held.tile([C, 4, P], F32, name=f"r{e}", tag=f"r{e}", align_bytes=64)
+            sums = banks[SUM_BANK[e]][:].rearrange("c (p t) -> c t p", t=4)
+            if e == RELU_ON_VECTOR:
+                nc.vector.tensor_scalar_max(relued[e][:], sums, 0.0)
+            else:
+                nc.scalar.activation(out=relued[e][:], in_=sums, func=ACT.Relu)
             for t in range(4):
-                nc.tensor.transpose(turned_bank(e)[:, t * C : (t + 1) * C], r[e][:, t, :], ident[:])
+                nc.tensor.transpose(banks[TURNED_BANK[e]][:, t * C : (t + 1) * C], relued[e][:, t, :], ident[:])
 
         def square(e):
             g, side = divmod(e, 2)
             if side == 0:
-                h[g] = held.tile([P, GROUP, 4], BF16, name=f"h{g}", tag=f"hidden{g}", align_bytes=64)
+                hidden[g] = held.tile([P, GROUP, 4], BF16, name=f"h{g}", tag=f"hidden{g}", align_bytes=64)
             nc.scalar.activation(
-                out=h[g][:, side * C : (side + 1) * C, :],
-                in_=turned_bank(e)[:].rearrange("p (t c) -> p c t", t=4),
+                out=hidden[g][:, side * C : (side + 1) * C, :],
+                in_=banks[TURNED_BANK[e]][:].rearrange("p (t c) -> p c t", t=4),
                 func=ACT.Square,
             )
 
-        def quantise_h(g):
-            h_words[g] = held.tile([P, GROUP], U32, name=f"h_words{g}", tag=(f"h_words{g}" if g else "w1e2"), align_bytes=64)
-            nc.vector.quantize_mx(out=h_words[g][:].bitcast(FP8X4), scales=h_scales[g][:], in_=h[g][:].rearrange("p c t -> p (c t)"))
+        def quantise_hidden(g):
+            slot = f"h_words{g}" if g > 0 else "w1e2"
+            hidden_words[g] = held.tile([P, GROUP], U32, name=f"h_words{g}", tag=slot, align_bytes=64)
+            nc.vector.quantize_mx(out=hidden_words[g][:].bitcast(FP8X4), scales=hidden_scales[g][:], in_=hidden[g][:].rearrange("p c t -> p (c t)"))
 
         def second_layer(g):
             for side in range(2):
@@ -258,10 +273,10 @@ def tile_moe_pln_mlp_relu2_kernel(tc, xT, w1_words, w1_scales, w2_words, w2_scal
                 cols = slice(side * C, (side + 1) * C)
                 nc.tensor.matmul_mx(
                     out=y_bank(g)[:, cols],
-                    lhsT=w2w[e].bitcast(FP4X4),
-                    lhsT_scale=w2s[:, e * N : (e + 1) * N],
-                    rhs=h_words[g][:, cols].bitcast(FP8X4),
-                    rhs_scale=h_scales[g][:, cols],
+                    lhsT=w2_code[e].bitcast(FP4X4),
+                    lhsT_scale=w2_scale[:, e * N : (e + 1) * N],
+                    rhs=hidden_words[g][:, cols].bitcast(FP8X4),
+                    rhs_scale=hidden_scales[g][:, cols],
                     start=True,
                     stop=True,
                 )
@@ -272,42 +287,38 @@ def tile_moe_pln_mlp_relu2_kernel(tc, xT, w1_words, w1_scales, w2_words, w2_scal
             picked = offsets[:, g * GROUP // 16 : (g + 1) * GROUP // 16]
             nc.vector.tensor_tensor(out_sb[:].indirect(picked), y_sb[:], gate_sb[:, g * GROUP : (g + 1) * GROUP], MULT)
 
-        def both_passes(e):
-            for s in range(PASSES):
-                first_layer(e, s)
+        def both_experts(work, g):
+            work(2 * g)
+            work(2 * g + 1)
 
-        both_passes(0)
-        both_passes(1)
-
-        def step(e):
-            relu(e)
-            turn(e)
-            if e + 3 < E:
-                both_passes(e + 3)
-
-        both_passes(2)
-        step(0)
-        step(1)
-        square(0)
-        square(1)
-        quantise_h(0)
-        quantise_group(GROUPS - 1, "hidden0")
+        for s in range(PASSES):
+            for e in range(2):
+                first_layer_pass(e, s)
+        both_experts(relu_and_turn, 0)
+        both_experts(first_layer, 1)
+        both_experts(square, 0)
+        quantise_hidden(0)
+        quantise_both_passes(3, "hidden0")
         second_layer(0)
-        step(2)
-        step(3)
-        for e in range(2, E):
-            if e + 2 < E:
-                step(e + 2)
-            square(e)
-            if e == 2:
-                put_back(0)
-            if e == E - 2:
-                second_layer(GROUPS - 2)
-            if e % 2:
-                quantise_h(e // 2)
-                if e != E - 3:
-                    second_layer(e // 2)
-                if e > 3:
-                    put_back(e // 2 - 1)
-        put_back(GROUPS - 1)
+
+        both_experts(first_layer, 2)
+        both_experts(relu_and_turn, 1)
+        put_back(0)
+        both_experts(relu_and_turn, 2)
+        both_experts(square, 1)
+        quantise_hidden(1)
+        both_experts(first_layer, 3)
+        second_layer(1)
+        both_experts(square, 2)
+        quantise_hidden(2)
+
+        both_experts(relu_and_turn, 3)
+        put_back(1)
+        square(E - 2)
+        second_layer(2)
+        square(E - 1)
+        quantise_hidden(3)
+        second_layer(3)
+        put_back(2)
+        put_back(3)
         nc.sync.dma_start(out=out, in_=out_sb[:])

@@ -24,15 +24,13 @@ GROUP = 2 * C
 GROUPS = SLOTS // GROUP
 
 CHUNKS = (
-    (0, 0, 1024, 640),
-    (0, 1024, 1024, 640),
-    (1, 0, 1024, 0),
-    (1, 1024, 1024, 640),
+    (0, 0, 2048, 1344),
+    (1, 0, 2048, 1344),
     (2, 0, 1024, 0),
-    (2, 1024, 1024, 640),
+    (2, 1024, 1024, 448),
     (3, 0, 1024, 0),
-    (3, 1024, 512, 512),
-    (3, 1536, 512, 320),
+    (3, 1024, 640, 640),
+    (3, 1664, 384, 256),
 )
 
 SCALE_RUNS = ((0, 2), (2, E))
@@ -141,7 +139,7 @@ def tile_moe_pln_mlp_relu2_kernel(tc, xT, w1_words, w1_scales, w2_words, w2_scal
             for j in range(4):
                 column = gate_cols[:, 4 * half + j : 4 * half + j + 1].to_broadcast([P, P])
                 nc.tensor.transpose(bank[:, j * P : (j + 1) * P], column, ident[:])
-            nc.vector.tensor_copy(
+            nc.scalar.copy(
                 gate_sb[:].rearrange("n (p half j) -> n half p j", half=2, j=4)[:, half],
                 bank[:].rearrange("n (j p) -> n p j", j=4),
             )

@@ -33,7 +33,7 @@ CHUNKS = (
     (3, 1664, 384, 256),
 )
 
-SCALE_RUNS = ((0, 2), (2, E))
+SCALE_RUNS = ((0, 7), (7, E * PASSES))
 
 THIRD_PAIR_BLOCK = {1: 2, 2: 1, 3: 0}
 LAST_PAIR_BLOCK = {1: 3, 2: 4, 3: 2}
@@ -42,7 +42,7 @@ SUM_BANK = (0, 1, 2, 3, 0, 1, 1, 5)
 TURNED_BANK = (4, 5, 4, 5, 2, 3, 4, 0)
 SPARE_BANK = 6
 
-RELU_ON_VECTOR = 6
+RELU_ON_VECTOR = (4, 6)
 
 
 def tile_moe_pln_mlp_relu2_kernel(tc, xT, w1_words, w1_scales, w2_words, w2_scales, gate, offs, out):
@@ -55,16 +55,16 @@ def tile_moe_pln_mlp_relu2_kernel(tc, xT, w1_words, w1_scales, w2_words, w2_scal
 
         offsets = lists.tile([P, SLOTS // 16], U16, name="offsets")
 
-        w1_scale_tiles = [held.tile([P, (last - first) * PASSES * H], U8, name=f"w1s{first}", align_bytes=64) for first, last in SCALE_RUNS]
+        w1_scale_tiles = [held.tile([P, (last - first) * H], U8, name=f"w1s{first}", align_bytes=64) for first, last in SCALE_RUNS]
         w1_scale = {
-            e: tile[:, (e - first) * PASSES * H : (e - first + 1) * PASSES * H]
+            divmod(j, PASSES): tile[:, (j - first) * H : (j - first + 1) * H]
             for tile, (first, last) in zip(w1_scale_tiles, SCALE_RUNS)
-            for e in range(first, last)
+            for j in range(first, last)
         }
         w2_scale = held.tile([P, E * N], U8, name="w2s", align_bytes=64)
         nc.vector.memset(w1_scale_tiles[0][:].bitcast(I32), 0)
         long_run = w1_scale_tiles[1][:].bitcast(I32)
-        a_third = long_run.shape[1] // 3
+        a_third = long_run.shape[1] // 9
         nc.vector.memset(long_run[:, :a_third], 0)
         nc.gpsimd.memset(long_run[:, a_third:], 0)
         nc.vector.memset(w2_scale[:].bitcast(I32), 0)
@@ -92,20 +92,21 @@ def tile_moe_pln_mlp_relu2_kernel(tc, xT, w1_words, w1_scales, w2_words, w2_scal
 
         def load_w1_scales(run):
             first, last = SCALE_RUNS[run]
-            rows = w1_scale_tiles[run][:].bitcast(I32).rearrange("p (e b) -> p e b", e=(last - first) * PASSES)
+            rows = w1_scale_tiles[run][:].bitcast(I32).rearrange("p (e b) -> p e b", e=last - first)
             for r in range(4):
-                nc.sync.dma_start(out=rows[r:P:32], in_=w1_scales_int[r][:, first * PASSES : last * PASSES, :])
+                nc.sync.dma_start(out=rows[r:P:32], in_=w1_scales_int[r][:, first:last, :])
 
         def load_w2_scales():
             rows = w2_scale[:].bitcast(I32).rearrange("p (e b) -> p e b", e=E)
             for r in range(4):
                 nc.sync.dma_start(out=rows[r:P:32], in_=w2_scales_int[r])
 
-        def load_w1_first_group(s):
-            tile = held.tile([P, 2 * 2 * H], U8, name=f"w1p{s}", align_bytes=64)
-            nc.sync.dma_start(out=tile[:].bitcast(I32).rearrange("p (e b) -> p e b", e=2), in_=w1_words_int[:, s : 2 * PASSES : PASSES, :])
-            for e in range(2):
-                w1_code[e, s] = tile[:, e * 2 * H : (e + 1) * 2 * H]
+        def load_w1_pass(g, s):
+            tile = held.tile([P, 2 * 2 * H], U8, name=f"w1g{g}p{s}", tag=f"w1g{g}p{s}", align_bytes=64)
+            first = 2 * g * PASSES + s
+            nc.sync.dma_start(out=tile[:].bitcast(I32).rearrange("p (e b) -> p e b", e=2), in_=w1_words_int[:, first : first + 2 * PASSES - s : PASSES, :])
+            for side in range(2):
+                w1_code[2 * g + side, s] = tile[:, side * 2 * H : (side + 1) * 2 * H]
 
         def load_w1(e):
             tile = held.tile([P, PASSES * 2 * H], U8, name=f"w1e{e}", tag=f"w1e{e}", align_bytes=64)
@@ -121,11 +122,13 @@ def tile_moe_pln_mlp_relu2_kernel(tc, xT, w1_words, w1_scales, w2_words, w2_scal
 
         load_w1_scales(0)
         for s in range(PASSES):
-            load_w1_first_group(s)
+            load_w1_pass(0, s)
+        load_w1_pass(1, 0)
         load_w2_scales()
         load_w2(0, 2)
         load_w1_scales(1)
-        for e in range(2, E):
+        load_w1_pass(1, 1)
+        for e in range(4, E):
             load_w1(e)
         load_w2(2, E)
 
@@ -231,7 +234,7 @@ def tile_moe_pln_mlp_relu2_kernel(tc, xT, w1_words, w1_scales, w2_words, w2_scal
                 lhsT=words[s, e].bitcast(FP8X4),
                 lhsT_scale=scales[s, e],
                 rhs=w1_code[e, s].bitcast(FP4X4),
-                rhs_scale=w1_scale[e][:, s * H : (s + 1) * H],
+                rhs_scale=w1_scale[e, s],
                 start=(s == 0),
                 stop=(s == PASSES - 1),
             )
@@ -243,7 +246,7 @@ def tile_moe_pln_mlp_relu2_kernel(tc, xT, w1_words, w1_scales, w2_words, w2_scal
         def relu_and_turn(e):
             relued[e] = held.tile([C, 4, P], F32, name=f"r{e}", tag=f"r{e}", align_bytes=64)
             sums = banks[SUM_BANK[e]][:].rearrange("c (p t) -> c t p", t=4)
-            if e == RELU_ON_VECTOR:
+            if e in RELU_ON_VECTOR:
                 nc.vector.tensor_scalar_max(relued[e][:], sums, 0.0)
             else:
                 nc.scalar.activation(out=relued[e][:], in_=sums, func=ACT.Relu)
@@ -261,7 +264,7 @@ def tile_moe_pln_mlp_relu2_kernel(tc, xT, w1_words, w1_scales, w2_words, w2_scal
             )
 
         def quantise_hidden(g):
-            slot = f"h_words{g}" if g > 0 else "w1e2"
+            slot = f"h_words{g}" if g > 0 else "w1g1p1"
             hidden_words[g] = held.tile([P, GROUP], U32, name=f"h_words{g}", tag=slot, align_bytes=64)
             nc.vector.quantize_mx(out=hidden_words[g][:].bitcast(FP8X4), scales=hidden_scales[g][:], in_=hidden[g][:].rearrange("p c t -> p (c t)"))
 
@@ -293,7 +296,9 @@ def tile_moe_pln_mlp_relu2_kernel(tc, xT, w1_words, w1_scales, w2_words, w2_scal
             for e in range(2):
                 first_layer_pass(e, s)
         both_experts(relu_and_turn, 0)
-        both_experts(first_layer, 1)
+        for s in range(PASSES):
+            for e in range(2, 4):
+                first_layer_pass(e, s)
         both_experts(square, 0)
         quantise_hidden(0)
         quantise_both_passes(3, "hidden0")
@@ -301,8 +306,9 @@ def tile_moe_pln_mlp_relu2_kernel(tc, xT, w1_words, w1_scales, w2_words, w2_scal
 
         both_experts(first_layer, 2)
         both_experts(relu_and_turn, 1)
+        relu_and_turn(4)
         put_back(0)
-        both_experts(relu_and_turn, 2)
+        relu_and_turn(5)
         both_experts(square, 1)
         quantise_hidden(1)
         both_experts(first_layer, 3)

@@ -27,10 +27,10 @@ CHUNKS = (
     (0, 0, 2048, 1344),
     (1, 0, 2048, 1344),
     (2, 0, 1024, 0),
-    (2, 1024, 1024, 448),
-    (3, 0, 1024, 0),
-    (3, 1024, 640, 640),
-    (3, 1664, 384, 256),
+    (2, 1024, 1024, 512),
+    (3, 0, 896, 0),
+    (3, 896, 768, 448),
+    (3, 1664, 384, 224),
 )
 
 SCALE_RUNS = ((0, 7), (7, E * PASSES))
@@ -164,8 +164,8 @@ def tile_moe_pln_mlp_relu2_kernel(tc, xT, w1_words, w1_scales, w2_words, w2_scal
         def gather(dst, u, first, count):
             nc.vector.tensor_copy(dst, pairs[u][:].bitcast(U32).indirect(offsets[:, first // 16 : (first + count) // 16]))
 
-        def weave_first_pass(g, slot):
-            both_woven[g] = held.tile([P, PASSES * 4 * GROUP], BF16, name=f"woven_{g}", tag=slot, align_bytes=64)
+        def weave_first_pass(g, tile):
+            both_woven[g] = tile[:, (g - 2) * PASSES * 4 * GROUP : (g - 1) * PASSES * 4 * GROUP]
             second_pass_woven[g] = both_woven[g][:, 4 * GROUP :]
             src = first_pass_runs[:].rearrange("p (v c) -> p c v", v=2)[:, (g - 2) * GROUP : (g - 1) * GROUP, :]
             nc.scalar.copy(by_pair(both_woven[g][:, : 4 * GROUP], U32), src)
@@ -185,7 +185,7 @@ def tile_moe_pln_mlp_relu2_kernel(tc, xT, w1_words, w1_scales, w2_words, w2_scal
                 scales[key] = scale_bytes[:, a * C : (a + 1) * C]
 
         def quantise_both_passes(g, slot):
-            quantise_tokens([(s, e) for s in range(PASSES) for e in (2 * g, 2 * g + 1)], both_woven[g][:], slot)
+            quantise_tokens([(s, e) for s in range(PASSES) for e in (2 * g, 2 * g + 1)], both_woven[g], slot)
 
         for i, (u, t0, width, by_vector) in enumerate(CHUNKS):
             dst = pairs[u][:, 2 * t0 : 2 * (t0 + width)].rearrange("p (c i j) -> p c j i", i=4, j=2)
@@ -207,8 +207,9 @@ def tile_moe_pln_mlp_relu2_kernel(tc, xT, w1_words, w1_scales, w2_words, w2_scal
                 for g in range(1, GROUPS):
                     gather(block(THIRD_PAIR_BLOCK[g]), u, g * GROUP, GROUP)
 
-        for g, chunk in ((2, len(CHUNKS) - 2), (3, len(CHUNKS) - 1)):
-            weave_first_pass(g, f"raw{chunk}")
+        late_woven = held.tile([P, 2 * PASSES * 4 * GROUP], BF16, name="late_woven", tag=f"raw{len(CHUNKS) - 1}", align_bytes=64)
+        for g in (2, 3):
+            weave_first_pass(g, late_woven)
 
         last = 2 * PASSES - 1
         gather(by_pair(second_pass_woven[0], U32)[:, :, 1], last, 0, GROUP)

@@ -28,21 +28,19 @@ CHUNKS = (
     (1, 0, 2048, 1344),
     (2, 0, 1024, 0),
     (2, 1024, 1024, 512),
-    (3, 0, 896, 0),
-    (3, 896, 768, 448),
-    (3, 1664, 384, 224),
+    (3, 0, 1024, 0),
+    (3, 1024, 512, 320),
+    (3, 1536, 512, 352),
 )
 
 SCALE_RUNS = ((0, 7), (7, E * PASSES))
-
-THIRD_PAIR_BLOCK = {1: 2, 2: 1, 3: 0}
-LAST_PAIR_BLOCK = {1: 3, 2: 4, 3: 2}
 
 SUM_BANK = (0, 1, 2, 3, 0, 1, 1, 5)
 TURNED_BANK = (4, 5, 4, 5, 2, 3, 4, 0)
 SPARE_BANK = 6
 
 RELU_ON_VECTOR = (4, 6)
+RELU_IN_HALVES = (0, 1, 7)
 
 
 def tile_moe_pln_mlp_relu2_kernel(tc, xT, w1_words, w1_scales, w2_words, w2_scales, gate, offs, out):
@@ -63,10 +61,10 @@ def tile_moe_pln_mlp_relu2_kernel(tc, xT, w1_words, w1_scales, w2_words, w2_scal
         }
         w2_scale = held.tile([P, E * N], U8, name="w2s", align_bytes=64)
         nc.vector.memset(w1_scale_tiles[0][:].bitcast(I32), 0)
-        long_run = w1_scale_tiles[1][:].bitcast(I32)
-        a_third = long_run.shape[1] // 9
-        nc.vector.memset(long_run[:, :a_third], 0)
-        nc.gpsimd.memset(long_run[:, a_third:], 0)
+        second_run = w1_scale_tiles[1][:].bitcast(I32)
+        a_ninth = second_run.shape[1] // 9
+        nc.vector.memset(second_run[:, :a_ninth], 0)
+        nc.gpsimd.memset(second_run[:, a_ninth:], 0)
         nc.vector.memset(w2_scale[:].bitcast(I32), 0)
 
         x_rows = xT.rearrange("(s p t) token -> s p t token", s=PASSES, t=4)
@@ -150,13 +148,10 @@ def tile_moe_pln_mlp_relu2_kernel(tc, xT, w1_words, w1_scales, w2_words, w2_scal
         pairs = [held.tile([P, 2 * T], BF16, name=f"pairs{u}", align_bytes=64) for u in range(2 * PASSES)]
         first_pass_woven = held.tile([P, 4 * 2 * GROUP], BF16, name="front", align_bytes=64)
         first_pass_runs = held.tile([P, 2 * 2 * GROUP], U32, name="planes", align_bytes=64)
-        blocks = held.tile([P, 5 * GROUP], U32, name="late", align_bytes=64)
+        blocks = held.tile([P, 6 * GROUP], U32, name="late", align_bytes=64)
         group1_woven = held.tile([P, 4 * GROUP], BF16, name="second_woven", align_bytes=64)
-        second_pass_woven = {0: blocks[:, 3 * GROUP :].bitcast(BF16), 1: group1_woven[:]}
+        second_pass_woven = {0: blocks[:, 3 * GROUP : 5 * GROUP].bitcast(BF16), 1: group1_woven[:]}
         words, scales, both_woven = {}, {}, {}
-
-        def block(b):
-            return blocks[:, b * GROUP : (b + 1) * GROUP]
 
         def by_pair(woven, dtype):
             return woven.bitcast(dtype).rearrange("p (c v) -> p c v", v=2)
@@ -171,9 +166,8 @@ def tile_moe_pln_mlp_relu2_kernel(tc, xT, w1_words, w1_scales, w2_words, w2_scal
             nc.scalar.copy(by_pair(both_woven[g][:, : 4 * GROUP], U32), src)
 
         def weave_second_pass(g):
-            low, high = THIRD_PAIR_BLOCK[g], LAST_PAIR_BLOCK[g]
-            src = blocks[:].bitcast(I32).rearrange("p (b c) -> p b c", c=GROUP)[:, low : high + 1 : high - low, :]
-            nc.vector.tensor_copy(by_pair(second_pass_woven[g], I32), src.rearrange("p v c -> p c v"))
+            src = blocks[:].rearrange("p (b c) -> p b c", c=GROUP)[:, g - 1 : g + 3 : 3, :].rearrange("p v c -> p c v")
+            nc.vector.tensor_copy(by_pair(second_pass_woven[g], I32), src.bitcast(I32))
 
         def quantise_tokens(keys, woven, slot):
             count = C * len(keys)
@@ -204,8 +198,7 @@ def tile_moe_pln_mlp_relu2_kernel(tc, xT, w1_words, w1_scales, w2_words, w2_scal
                 quantise_tokens([(0, e) for e in range(4)], first_pass_woven[:], "front_codes")
             if u == 2:
                 gather(by_pair(second_pass_woven[0], U32)[:, :, 0], u, 0, GROUP)
-                for g in range(1, GROUPS):
-                    gather(block(THIRD_PAIR_BLOCK[g]), u, g * GROUP, GROUP)
+                gather(blocks[:, : 3 * GROUP], u, GROUP, 3 * GROUP)
 
         late_woven = held.tile([P, 2 * PASSES * 4 * GROUP], BF16, name="late_woven", tag=f"raw{len(CHUNKS) - 1}", align_bytes=64)
         for g in (2, 3):
@@ -214,14 +207,12 @@ def tile_moe_pln_mlp_relu2_kernel(tc, xT, w1_words, w1_scales, w2_words, w2_scal
         last = 2 * PASSES - 1
         gather(by_pair(second_pass_woven[0], U32)[:, :, 1], last, 0, GROUP)
         quantise_tokens([(1, 0), (1, 1)], second_pass_woven[0], "first")
-        gather(block(LAST_PAIR_BLOCK[1]), last, GROUP, GROUP)
-        weave_second_pass(1)
-        gather(block(LAST_PAIR_BLOCK[2]), last, 2 * GROUP, GROUP)
-        quantise_tokens([(1, 2), (1, 3)], second_pass_woven[1], "second")
-        gather(block(LAST_PAIR_BLOCK[3]), last, 3 * GROUP, GROUP)
-        for g in range(2, GROUPS):
+        gather(blocks[:, 3 * GROUP :], last, GROUP, 3 * GROUP)
+        for g in range(1, 3):
             weave_second_pass(g)
+        quantise_tokens([(1, 2), (1, 3)], second_pass_woven[1], "second")
         quantise_both_passes(2, "group2")
+        weave_second_pass(3)
 
         relued, hidden, hidden_words = {}, {}, {}
         hidden_scales = [held.tile([P, GROUP], U8, name=f"h_scales{g}", align_bytes=64) for g in range(GROUPS)]
@@ -249,6 +240,9 @@ def tile_moe_pln_mlp_relu2_kernel(tc, xT, w1_words, w1_scales, w2_words, w2_scal
             sums = banks[SUM_BANK[e]][:].rearrange("c (p t) -> c t p", t=4)
             if e in RELU_ON_VECTOR:
                 nc.vector.tensor_scalar_max(relued[e][:], sums, 0.0)
+            elif e in RELU_IN_HALVES:
+                for half in (slice(0, 2), slice(2, 4)):
+                    nc.scalar.activation(out=relued[e][:, half], in_=sums[:, half], func=ACT.Relu)
             else:
                 nc.scalar.activation(out=relued[e][:], in_=sums, func=ACT.Relu)
             for t in range(4):
@@ -267,7 +261,8 @@ def tile_moe_pln_mlp_relu2_kernel(tc, xT, w1_words, w1_scales, w2_words, w2_scal
         def quantise_hidden(g):
             slot = f"h_words{g}" if g > 0 else "w1g1p1"
             hidden_words[g] = held.tile([P, GROUP], U32, name=f"h_words{g}", tag=slot, align_bytes=64)
-            nc.vector.quantize_mx(out=hidden_words[g][:].bitcast(FP8X4), scales=hidden_scales[g][:], in_=hidden[g][:].rearrange("p c t -> p (c t)"))
+            for cols in ((slice(0, C), slice(C, GROUP)) if g == 0 else (slice(0, GROUP),)):
+                nc.vector.quantize_mx(out=hidden_words[g][:, cols].bitcast(FP8X4), scales=hidden_scales[g][:, cols], in_=hidden[g][:, cols].rearrange("p c t -> p (c t)"))
 
         def second_layer(g):
             for side in range(2):

@@ -20,27 +20,15 @@ MULT = mybir.AluOpType.mult
 
 P = 128
 PASSES = K // 512
+ROWS = 4 * PASSES
 GROUP = 2 * C
 GROUPS = SLOTS // GROUP
 
-CHUNKS = (
-    (0, 0, 2048, 1344),
-    (1, 0, 2048, 1344),
-    (2, 0, 1024, 0),
-    (2, 1024, 1024, 512),
-    (3, 0, 1024, 0),
-    (3, 1024, 512, 320),
-    (3, 1536, 512, 352),
-)
-
-SCALE_RUNS = ((0, 7), (7, E * PASSES))
-
-SUM_BANK = (0, 1, 2, 3, 0, 1, 1, 5)
-TURNED_BANK = (4, 5, 4, 5, 2, 3, 4, 0)
-SPARE_BANK = 6
-
-RELU_ON_VECTOR = (4, 6)
-RELU_IN_HALVES = (0, 1, 7)
+SUM_BANK = (0, 1, 2, 3, 1, 2, 3, 2)
+TURNED_BANK = (4, 5, 6, 0, 5, 6, 0, 1)
+Y_BANK = (7, 3, 7, 4)
+GATE_BANKS = (6, 7)
+RELU_ON_VECTOR = (1, 3, 4, 7)
 
 
 def tile_moe_pln_mlp_relu2_kernel(tc, xT, w1_words, w1_scales, w2_words, w2_scales, gate, offs, out):
@@ -50,36 +38,35 @@ def tile_moe_pln_mlp_relu2_kernel(tc, xT, w1_words, w1_scales, w2_words, w2_scal
         held = ctx.enter_context(tc.tile_pool(name="held", bufs=1))
         psum = ctx.enter_context(tc.psum_pool(name="psum", bufs=1))
         banks = [psum.tile([P, 512], F32, name=f"bank{b}") for b in range(8)]
-
         offsets = lists.tile([P, SLOTS // 16], U16, name="offsets")
 
-        w1_scale_tiles = [held.tile([P, (last - first) * H], U8, name=f"w1s{first}", align_bytes=64) for first, last in SCALE_RUNS]
+        def sbuf(shape, dtype, name, slot=None):
+            return held.tile(shape, dtype, name=name, tag=slot or name, align_bytes=64)
+
+        scale_runs = ((0, 2), (2, 4), (4, 8))
+        w1_scale_tiles = [sbuf([P, (last - first) * PASSES * H], U8, f"w1s{first}") for first, last in scale_runs]
         w1_scale = {
-            divmod(j, PASSES): tile[:, (j - first) * H : (j - first + 1) * H]
-            for tile, (first, last) in zip(w1_scale_tiles, SCALE_RUNS)
-            for j in range(first, last)
+            (e, s): tile[:, ((e - first) * PASSES + s) * H : ((e - first) * PASSES + s + 1) * H]
+            for tile, (first, last) in zip(w1_scale_tiles, scale_runs)
+            for e in range(first, last)
+            for s in range(PASSES)
         }
-        w2_scale = held.tile([P, E * N], U8, name="w2s", align_bytes=64)
-        nc.vector.memset(w1_scale_tiles[0][:].bitcast(I32), 0)
-        second_run = w1_scale_tiles[1][:].bitcast(I32)
-        a_ninth = second_run.shape[1] // 9
-        nc.vector.memset(second_run[:, :a_ninth], 0)
-        nc.gpsimd.memset(second_run[:, a_ninth:], 0)
-        nc.vector.memset(w2_scale[:].bitcast(I32), 0)
+        w2_scale = sbuf([P, E * N], U8, "w2s")
+        for tile in w1_scale_tiles + [w2_scale]:
+            nc.vector.memset(tile[:].bitcast(I32), 0)
 
-        x_rows = xT.rearrange("(s p t) token -> s p t token", s=PASSES, t=4)
-        raws = []
-        for i, (u, t0, width, by_vector) in enumerate(CHUNKS):
-            s, v = divmod(u, 2)
-            raw = held.tile([P, 2, width], F32, name=f"raw{i}", tag=f"raw{i}", align_bytes=64)
-            nc.sync.dma_start(out=raw[:], in_=x_rows[s][:, 2 * v : 2 * v + 2, t0 : t0 + width])
-            raws.append(raw)
-            if i == 0:
-                gate_cols = held.tile([P, SLOTS // P], F32, name="gate_cols")
-                nc.sync.dma_start(out=gate_cols[:], in_=gate[0].rearrange("(p j) -> p j", p=P))
+        x_rows = xT.rearrange("(s p t) token -> s t p token", s=PASSES, t=4)
+        rows = []
+        for r in range(ROWS):
+            row = sbuf([P, T], F32, f"row{r}")
+            nc.sync.dma_start(out=row[:], in_=x_rows[r // 4][r % 4])
+            rows.append(row)
+            if r == 0:
                 nc.sync.dma_start(offsets[:], offs)
+                gate_cols = sbuf([P, SLOTS // P], F32, "gate_cols")
+                nc.sync.dma_start(out=gate_cols[:], in_=gate[0].rearrange("(p j) -> p j", p=P))
 
-        ident = held.tile([P, P], F32, name="ident")
+        ident = sbuf([P, P], F32, "ident")
         make_identity(nc, ident[:])
 
         w1_words_int = w1_words.bitcast(I32).rearrange("e s p b -> p (e s) b")
@@ -89,142 +76,114 @@ def tile_moe_pln_mlp_relu2_kernel(tc, xT, w1_words, w1_scales, w2_words, w2_scal
         w1_code, w2_code = {}, {}
 
         def load_w1_scales(run):
-            first, last = SCALE_RUNS[run]
-            rows = w1_scale_tiles[run][:].bitcast(I32).rearrange("p (e b) -> p e b", e=last - first)
+            first, last = scale_runs[run]
+            dst = w1_scale_tiles[run][:].bitcast(I32).rearrange("p (j b) -> p j b", j=(last - first) * PASSES)
             for r in range(4):
-                nc.sync.dma_start(out=rows[r:P:32], in_=w1_scales_int[r][:, first:last, :])
+                nc.sync.dma_start(out=dst[r:P:32], in_=w1_scales_int[r][:, first * PASSES : last * PASSES, :])
 
         def load_w2_scales():
-            rows = w2_scale[:].bitcast(I32).rearrange("p (e b) -> p e b", e=E)
+            dst = w2_scale[:].bitcast(I32).rearrange("p (e b) -> p e b", e=E)
             for r in range(4):
-                nc.sync.dma_start(out=rows[r:P:32], in_=w2_scales_int[r])
+                nc.sync.dma_start(out=dst[r:P:32], in_=w2_scales_int[r])
 
-        def load_w1_pass(g, s):
-            tile = held.tile([P, 2 * 2 * H], U8, name=f"w1g{g}p{s}", tag=f"w1g{g}p{s}", align_bytes=64)
-            first = 2 * g * PASSES + s
-            nc.sync.dma_start(out=tile[:].bitcast(I32).rearrange("p (e b) -> p e b", e=2), in_=w1_words_int[:, first : first + 2 * PASSES - s : PASSES, :])
-            for side in range(2):
-                w1_code[2 * g + side, s] = tile[:, side * 2 * H : (side + 1) * 2 * H]
-
-        def load_w1(e):
-            tile = held.tile([P, PASSES * 2 * H], U8, name=f"w1e{e}", tag=f"w1e{e}", align_bytes=64)
-            nc.sync.dma_start(out=tile[:].bitcast(I32).rearrange("p (s b) -> p s b", s=PASSES), in_=w1_words_int[:, PASSES * e : PASSES * (e + 1), :])
-            for s in range(PASSES):
-                w1_code[e, s] = tile[:, s * 2 * H : (s + 1) * 2 * H]
+        def load_w1(keys):
+            js = [PASSES * e + s for e, s in keys]
+            step = js[1] - js[0]
+            tile = sbuf([P, len(keys) * 2 * H], U8, f"w1_{js[0]}")
+            nc.sync.dma_start(out=tile[:].bitcast(I32).rearrange("p (j b) -> p j b", j=len(keys)), in_=w1_words_int[:, js[0] : js[-1] + 1 : step, :])
+            for a, key in enumerate(keys):
+                w1_code[key] = tile[:, a * 2 * H : (a + 1) * 2 * H]
 
         def load_w2(first, last):
-            tile = held.tile([P, (last - first) * 2 * N], U8, name=f"w2w{first}", align_bytes=64)
+            tile = sbuf([P, (last - first) * 2 * N], U8, f"w2_{first}")
             nc.sync.dma_start(out=tile[:].bitcast(I32).rearrange("p (e b) -> p e b", e=last - first), in_=w2_words_int[:, first:last, :])
             for e in range(first, last):
                 w2_code[e] = tile[:, (e - first) * 2 * N : (e - first + 1) * 2 * N]
 
         load_w1_scales(0)
         for s in range(PASSES):
-            load_w1_pass(0, s)
-        load_w1_pass(1, 0)
-        load_w2_scales()
-        load_w2(0, 2)
+            load_w1([(0, s), (1, s)])
         load_w1_scales(1)
-        load_w1_pass(1, 1)
-        for e in range(4, E):
-            load_w1(e)
-        load_w2(2, E)
+        load_w1([(e, s) for e in (2, 3) for s in range(PASSES)])
+        load_w2_scales()
+        load_w1_scales(2)
+        load_w1([(4, s) for s in range(PASSES)])
+        load_w2(0, 4)
+        for e in range(5, E):
+            load_w1([(e, s) for s in range(PASSES)])
+        load_w2(4, E)
 
-        out_sb = held.tile([P, T], F32, name="out_sb", align_bytes=64)
+        out_sb = sbuf([P, T], F32, "out_sb")
         for first in range(0, T, T // 2):
             nc.vector.memset(out_sb[:, first : first + T // 2], 0.0)
 
-        gate_sb = held.tile([P, SLOTS], F32, name="gate_sb", align_bytes=64)
+        gate_sb = sbuf([P, SLOTS], F32, "gate_sb")
         for half in range(2):
-            bank = banks[SPARE_BANK + half]
+            bank = banks[GATE_BANKS[half]]
             for j in range(4):
                 column = gate_cols[:, 4 * half + j : 4 * half + j + 1].to_broadcast([P, P])
                 nc.tensor.transpose(bank[:, j * P : (j + 1) * P], column, ident[:])
-            nc.scalar.copy(
-                gate_sb[:].rearrange("n (p half j) -> n half p j", half=2, j=4)[:, half],
-                bank[:].rearrange("n (j p) -> n p j", j=4),
+            nc.scalar.activation(
+                out=gate_sb[:].rearrange("n (p half j) -> n half p j", half=2, j=4)[:, half],
+                in_=bank[:].rearrange("n (j p) -> n p j", j=4),
+                func=ACT.Copy,
             )
 
-        pairs = [held.tile([P, 2 * T], BF16, name=f"pairs{u}", align_bytes=64) for u in range(2 * PASSES)]
-        first_pass_woven = held.tile([P, 4 * 2 * GROUP], BF16, name="front", align_bytes=64)
-        first_pass_runs = held.tile([P, 2 * 2 * GROUP], U32, name="planes", align_bytes=64)
-        blocks = held.tile([P, 6 * GROUP], U32, name="late", align_bytes=64)
-        group1_woven = held.tile([P, 4 * GROUP], BF16, name="second_woven", align_bytes=64)
-        second_pass_woven = {0: blocks[:, 3 * GROUP : 5 * GROUP].bitcast(BF16), 1: group1_woven[:]}
-        words, scales, both_woven = {}, {}, {}
+        def gather(engine, dst, r, first, count):
+            window = rows[r][:].indirect(offsets[:, first // 16 : (first + count) // 16])
+            if engine == "scalar":
+                nc.scalar.activation(out=dst, in_=window, func=ACT.Copy)
+            else:
+                nc.vector.tensor_copy(dst, window)
 
-        def by_pair(woven, dtype):
-            return woven.bitcast(dtype).rearrange("p (c v) -> p c v", v=2)
+        woven = [sbuf([P, 4 * SLOTS], BF16, f"woven{s}") for s in range(PASSES)]
 
-        def gather(dst, u, first, count):
-            nc.vector.tensor_copy(dst, pairs[u][:].bitcast(U32).indirect(offsets[:, first // 16 : (first + count) // 16]))
+        def weave(u, planes, first, count):
+            s, v = divmod(u, 2)
+            dst = woven[s][:, 4 * first : 4 * (first + count)].rearrange("p (c t) -> p c t", t=4)[:, :, 2 * v : 2 * v + 2]
+            nc.vector.tensor_copy(dst, planes.rearrange("p j c -> p c j"))
 
-        def weave_first_pass(g, tile):
-            both_woven[g] = tile[:, (g - 2) * PASSES * 4 * GROUP : (g - 1) * PASSES * 4 * GROUP]
-            second_pass_woven[g] = both_woven[g][:, 4 * GROUP :]
-            src = first_pass_runs[:].rearrange("p (v c) -> p c v", v=2)[:, (g - 2) * GROUP : (g - 1) * GROUP, :]
-            nc.scalar.copy(by_pair(both_woven[g][:, : 4 * GROUP], U32), src)
+        words, scales = {}, {}
 
-        def weave_second_pass(g):
-            src = blocks[:].rearrange("p (b c) -> p b c", c=GROUP)[:, g - 1 : g + 3 : 3, :].rearrange("p v c -> p c v")
-            nc.vector.tensor_copy(by_pair(second_pass_woven[g], I32), src.bitcast(I32))
+        def quantise_tokens(s, first, last, slot=None):
+            count = C * (last - first)
+            codes = sbuf([P, count], U32, f"words{s}_{first}", slot)
+            scale_bytes = sbuf([P, count], U8, f"scales{s}_{first}")
+            nc.vector.quantize_mx(out=codes[:].bitcast(FP8X4), scales=scale_bytes[:], in_=woven[s][:, 4 * C * first : 4 * C * last])
+            for e in range(first, last):
+                words[e, s] = codes[:, (e - first) * C : (e - first + 1) * C]
+                scales[e, s] = scale_bytes[:, (e - first) * C : (e - first + 1) * C]
 
-        def quantise_tokens(keys, woven, slot):
-            count = C * len(keys)
-            codes = held.tile([P, count], U32, name=f"words_{slot}", tag=slot, align_bytes=64)
-            scale_bytes = held.tile([P, count], U8, name=f"scales_{slot}", align_bytes=64)
-            nc.vector.quantize_mx(out=codes[:].bitcast(FP8X4), scales=scale_bytes[:], in_=woven)
-            for a, key in enumerate(keys):
-                words[key] = codes[:, a * C : (a + 1) * C]
-                scales[key] = scale_bytes[:, a * C : (a + 1) * C]
+        planes = [sbuf([P, 2, SLOTS], BF16, f"planes{u}") for u in range(3)]
+        for u in range(2):
+            gather("scalar", planes[u][:, 0, :], 2 * u, 0, SLOTS)
+            gather("vector", planes[u][:, 1, :], 2 * u + 1, 0, SLOTS)
+            weave(u, planes[u][:], 0, SLOTS)
+        for e in range(E):
+            quantise_tokens(0, e, e + 1)
+        half = SLOTS // 2
+        gather("scalar", planes[2][:, 0, :], 4, 0, SLOTS)
+        gather("scalar", planes[2][:, 1, :half], 5, 0, half)
+        gather("vector", planes[2][:, 1, half:], 5, half, half)
+        weave(2, planes[2][:], 0, SLOTS)
+        last_planes = sbuf([P, 7 * GROUP], BF16, "last_planes")
+        blocks = last_planes[:].rearrange("p (b c) -> p b c", c=GROUP)
+        gather("scalar", last_planes[:, : 3 * GROUP], 6, 0, 3 * GROUP)
+        gather("vector", blocks[:, 3, :], 6, 3 * GROUP, GROUP)
+        for g in range(GROUPS):
+            b = max(4, g + 3)
+            gather("scalar", blocks[:, b, :], 7, g * GROUP, GROUP)
+            weave(3, blocks[:, g : b + 1 : b - g, :], g * GROUP, GROUP)
+            if g < 2:
+                quantise_tokens(1, 2 * g, 2 * g + 2)
 
-        def quantise_both_passes(g, slot):
-            quantise_tokens([(s, e) for s in range(PASSES) for e in (2 * g, 2 * g + 1)], both_woven[g], slot)
-
-        for i, (u, t0, width, by_vector) in enumerate(CHUNKS):
-            dst = pairs[u][:, 2 * t0 : 2 * (t0 + width)].rearrange("p (c i j) -> p c j i", i=4, j=2)
-            src = raws[i][:].rearrange("p j (c i) -> p c j i", i=4)
-            cut = by_vector // 4
-            if by_vector > 0:
-                nc.vector.tensor_copy(dst[:, :cut], src[:, :cut])
-            if by_vector < width:
-                nc.scalar.activation(out=dst[:, cut:], in_=src[:, cut:], func=ACT.Copy)
-            if t0 + width < T:
-                continue
-            if u < 2:
-                gather(by_pair(first_pass_woven[:], U32)[:, :, u], u, 0, 2 * GROUP)
-                gather(first_pass_runs[:, u * 2 * GROUP : (u + 1) * 2 * GROUP], u, 2 * GROUP, 2 * GROUP)
-            if u == 1:
-                quantise_tokens([(0, e) for e in range(4)], first_pass_woven[:], "front_codes")
-            if u == 2:
-                gather(by_pair(second_pass_woven[0], U32)[:, :, 0], u, 0, GROUP)
-                gather(blocks[:, : 3 * GROUP], u, GROUP, 3 * GROUP)
-
-        late_woven = held.tile([P, 2 * PASSES * 4 * GROUP], BF16, name="late_woven", tag=f"raw{len(CHUNKS) - 1}", align_bytes=64)
-        for g in (2, 3):
-            weave_first_pass(g, late_woven)
-
-        last = 2 * PASSES - 1
-        gather(by_pair(second_pass_woven[0], U32)[:, :, 1], last, 0, GROUP)
-        quantise_tokens([(1, 0), (1, 1)], second_pass_woven[0], "first")
-        gather(blocks[:, 3 * GROUP :], last, GROUP, 3 * GROUP)
-        for g in range(1, 3):
-            weave_second_pass(g)
-        quantise_tokens([(1, 2), (1, 3)], second_pass_woven[1], "second")
-        quantise_both_passes(2, "group2")
-        weave_second_pass(3)
-
-        relued, hidden, hidden_words = {}, {}, {}
-        hidden_scales = [held.tile([P, GROUP], U8, name=f"h_scales{g}", align_bytes=64) for g in range(GROUPS)]
-
-        def y_bank(g):
-            return banks[TURNED_BANK[E - 2]] if g == GROUPS - 2 else banks[SPARE_BANK + g % 2]
+        relued, hidden, hidden_words, hidden_scales, y_sb = {}, {}, {}, {}, {}
 
         def first_layer_pass(e, s):
             nc.tensor.matmul_mx(
                 out=banks[SUM_BANK[e]][:],
-                lhsT=words[s, e].bitcast(FP8X4),
-                lhsT_scale=scales[s, e],
+                lhsT=words[e, s].bitcast(FP8X4),
+                lhsT_scale=scales[e, s],
                 rhs=w1_code[e, s].bitcast(FP4X4),
                 rhs_scale=w1_scale[e, s],
                 start=(s == 0),
@@ -235,23 +194,23 @@ def tile_moe_pln_mlp_relu2_kernel(tc, xT, w1_words, w1_scales, w2_words, w2_scal
             for s in range(PASSES):
                 first_layer_pass(e, s)
 
-        def relu_and_turn(e):
-            relued[e] = held.tile([C, 4, P], F32, name=f"r{e}", tag=f"r{e}", align_bytes=64)
+        def relu(e):
+            slot = {0: "words0_2", 1: "scales0_2"}.get(e)
+            relued[e] = sbuf([C, 4, P], F32, f"relued{e}", slot)
             sums = banks[SUM_BANK[e]][:].rearrange("c (p t) -> c t p", t=4)
             if e in RELU_ON_VECTOR:
                 nc.vector.tensor_scalar_max(relued[e][:], sums, 0.0)
-            elif e in RELU_IN_HALVES:
-                for half in (slice(0, 2), slice(2, 4)):
-                    nc.scalar.activation(out=relued[e][:, half], in_=sums[:, half], func=ACT.Relu)
             else:
                 nc.scalar.activation(out=relued[e][:], in_=sums, func=ACT.Relu)
+
+        def turn(e):
             for t in range(4):
                 nc.tensor.transpose(banks[TURNED_BANK[e]][:, t * C : (t + 1) * C], relued[e][:, t, :], ident[:])
 
         def square(e):
             g, side = divmod(e, 2)
             if side == 0:
-                hidden[g] = held.tile([P, GROUP, 4], BF16, name=f"h{g}", tag=f"hidden{g}", align_bytes=64)
+                hidden[g] = sbuf([P, GROUP, 4], BF16, f"hidden{g}")
             nc.scalar.activation(
                 out=hidden[g][:, side * C : (side + 1) * C, :],
                 in_=banks[TURNED_BANK[e]][:].rearrange("p (t c) -> p c t", t=4),
@@ -259,17 +218,17 @@ def tile_moe_pln_mlp_relu2_kernel(tc, xT, w1_words, w1_scales, w2_words, w2_scal
             )
 
         def quantise_hidden(g):
-            slot = f"h_words{g}" if g > 0 else "w1g1p1"
-            hidden_words[g] = held.tile([P, GROUP], U32, name=f"h_words{g}", tag=slot, align_bytes=64)
-            for cols in ((slice(0, C), slice(C, GROUP)) if g == 0 else (slice(0, GROUP),)):
-                nc.vector.quantize_mx(out=hidden_words[g][:, cols].bitcast(FP8X4), scales=hidden_scales[g][:, cols], in_=hidden[g][:, cols].rearrange("p c t -> p (c t)"))
+            slot = {0: "words0_4", 1: "words0_6"}.get(g)
+            hidden_words[g] = sbuf([P, GROUP], U32, f"h_words{g}", slot)
+            hidden_scales[g] = sbuf([P, GROUP], U8, f"h_scales{g}")
+            nc.vector.quantize_mx(out=hidden_words[g][:].bitcast(FP8X4), scales=hidden_scales[g][:], in_=hidden[g][:].rearrange("p c t -> p (c t)"))
 
         def second_layer(g):
             for side in range(2):
                 e = 2 * g + side
                 cols = slice(side * C, (side + 1) * C)
                 nc.tensor.matmul_mx(
-                    out=y_bank(g)[:, cols],
+                    out=banks[Y_BANK[g]][:, cols],
                     lhsT=w2_code[e].bitcast(FP4X4),
                     lhsT_scale=w2_scale[:, e * N : (e + 1) * N],
                     rhs=hidden_words[g][:, cols].bitcast(FP8X4),
@@ -278,47 +237,60 @@ def tile_moe_pln_mlp_relu2_kernel(tc, xT, w1_words, w1_scales, w2_words, w2_scal
                     stop=True,
                 )
 
-        def put_back(g):
-            y_sb = held.tile([P, GROUP], F32, name=f"y_sb{g}", align_bytes=64)
-            nc.scalar.copy(y_sb[:], y_bank(g)[:, :GROUP])
-            picked = offsets[:, g * GROUP // 16 : (g + 1) * GROUP // 16]
-            nc.vector.tensor_tensor(out_sb[:].indirect(picked), y_sb[:], gate_sb[:, g * GROUP : (g + 1) * GROUP], MULT)
+        def copy_y(g):
+            y_sb[g] = sbuf([P, GROUP], F32, f"y_sb{g}")
+            if g == 0:
+                nc.vector.tensor_copy(y_sb[g][:], banks[Y_BANK[g]][:, :GROUP])
+            else:
+                nc.scalar.copy(y_sb[g][:], banks[Y_BANK[g]][:, :GROUP])
 
-        def both_experts(work, g):
-            work(2 * g)
-            work(2 * g + 1)
+        def scatter(g):
+            picked = offsets[:, g * GROUP // 16 : (g + 1) * GROUP // 16]
+            nc.vector.tensor_tensor(out_sb[:].indirect(picked), y_sb[g][:], gate_sb[:, g * GROUP : (g + 1) * GROUP], MULT)
 
         for s in range(PASSES):
             for e in range(2):
                 first_layer_pass(e, s)
-        both_experts(relu_and_turn, 0)
-        for s in range(PASSES):
-            for e in range(2, 4):
-                first_layer_pass(e, s)
-        both_experts(square, 0)
+        first_layer(2)
+        first_layer(3)
+        for e in range(4):
+            relu(e)
+        quantise_tokens(1, 4, 6, "words0_3")
+        quantise_tokens(1, 6, 8, "words1_2")
+        for e in range(4):
+            turn(e)
+        for e in range(4):
+            square(e)
+        first_layer(4)
+        first_layer(5)
         quantise_hidden(0)
-        quantise_both_passes(3, "hidden0")
         second_layer(0)
-
-        both_experts(first_layer, 2)
-        both_experts(relu_and_turn, 1)
-        relu_and_turn(4)
-        put_back(0)
-        relu_and_turn(5)
-        both_experts(square, 1)
+        first_layer(6)
+        relu(4)
+        copy_y(0)
         quantise_hidden(1)
-        both_experts(first_layer, 3)
+        scatter(0)
+        relu(5)
+        relu(6)
+        turn(4)
+        turn(5)
+        first_layer(7)
         second_layer(1)
-        both_experts(square, 2)
+        relu(7)
+        square(4)
+        turn(6)
+        turn(7)
+        square(5)
+        copy_y(1)
         quantise_hidden(2)
-
-        both_experts(relu_and_turn, 3)
-        put_back(1)
-        square(E - 2)
+        scatter(1)
+        square(6)
+        square(7)
         second_layer(2)
-        square(E - 1)
         quantise_hidden(3)
+        copy_y(2)
         second_layer(3)
-        put_back(2)
-        put_back(3)
+        copy_y(3)
+        scatter(2)
+        scatter(3)
         nc.sync.dma_start(out=out, in_=out_sb[:])

@@ -25,10 +25,10 @@ GROUP = 2 * C
 GROUPS = SLOTS // GROUP
 
 SUM_BANK = (0, 1, 2, 3, 1, 2, 3, 2)
-TURNED_BANK = (4, 5, 6, 0, 5, 6, 0, 1)
-Y_BANK = (7, 3, 7, 4)
+TURNED_BANK = (4, 5, 6, 0, 7, 6, 0, 1)
+Y_BANK = (7, 3, 5, 4)
 GATE_BANKS = (6, 7)
-RELU_ON_VECTOR = (1, 3, 4, 7)
+RELU_ON_VECTOR = (1, 3, 4)
 
 
 def tile_moe_pln_mlp_relu2_kernel(tc, xT, w1_words, w1_scales, w2_words, w2_scales, gate, offs, out):
@@ -43,7 +43,7 @@ def tile_moe_pln_mlp_relu2_kernel(tc, xT, w1_words, w1_scales, w2_words, w2_scal
         def sbuf(shape, dtype, name, slot=None):
             return held.tile(shape, dtype, name=name, tag=slot or name, align_bytes=64)
 
-        scale_runs = ((0, 2), (2, 4), (4, 8))
+        scale_runs = ((0, 4), (4, 8))
         w1_scale_tiles = [sbuf([P, (last - first) * PASSES * H], U8, f"w1s{first}") for first, last in scale_runs]
         w1_scale = {
             (e, s): tile[:, ((e - first) * PASSES + s) * H : ((e - first) * PASSES + s + 1) * H]
@@ -52,19 +52,21 @@ def tile_moe_pln_mlp_relu2_kernel(tc, xT, w1_words, w1_scales, w2_words, w2_scal
             for s in range(PASSES)
         }
         w2_scale = sbuf([P, E * N], U8, "w2s")
+        out_sb = sbuf([P, T], F32, "out_sb")
+        nc.vector.memset(out_sb[:, : T // 2], 0.0)
+        nc.scalar.activation(out=out_sb[:, T // 2 :], in_=out_sb[:, : T // 2], func=ACT.Copy)
         for tile in w1_scale_tiles + [w2_scale]:
             nc.vector.memset(tile[:].bitcast(I32), 0)
 
-        x_rows = xT.rearrange("(s p t) token -> s t p token", s=PASSES, t=4)
+        gate_cols = sbuf([P, SLOTS // P], F32, "gate_cols")
+        nc.scalar.dma_start(out=gate_cols[:], in_=gate[0].rearrange("(p j) -> p j", p=P))
+        nc.sync.dma_start(offsets[:], offs)
+        x_rows = xT.rearrange("(s p t) token -> s p (t token)", s=PASSES, t=4)
         rows = []
-        for r in range(ROWS):
-            row = sbuf([P, T], F32, f"row{r}")
-            nc.sync.dma_start(out=row[:], in_=x_rows[r // 4][r % 4])
-            rows.append(row)
-            if r == 0:
-                nc.sync.dma_start(offsets[:], offs)
-                gate_cols = sbuf([P, SLOTS // P], F32, "gate_cols")
-                nc.sync.dma_start(out=gate_cols[:], in_=gate[0].rearrange("(p j) -> p j", p=P))
+        for r, count in ((0, 2), (2, 2), (4, 1), (5, 1), (6, 1), (7, 1)):
+            tile = sbuf([P, count * T], F32, f"row{r}")
+            nc.sync.dma_start(out=tile[:], in_=x_rows[r // 4][:, (r % 4) * T : (r % 4 + count) * T])
+            rows.extend(tile[:, a * T : (a + 1) * T] for a in range(count))
 
         ident = sbuf([P, P], F32, "ident")
         make_identity(nc, ident[:])
@@ -88,9 +90,8 @@ def tile_moe_pln_mlp_relu2_kernel(tc, xT, w1_words, w1_scales, w2_words, w2_scal
 
         def load_w1(keys):
             js = [PASSES * e + s for e, s in keys]
-            step = js[1] - js[0]
             tile = sbuf([P, len(keys) * 2 * H], U8, f"w1_{js[0]}")
-            nc.sync.dma_start(out=tile[:].bitcast(I32).rearrange("p (j b) -> p j b", j=len(keys)), in_=w1_words_int[:, js[0] : js[-1] + 1 : step, :])
+            nc.sync.dma_start(out=tile[:].bitcast(I32).rearrange("p (j b) -> p j b", j=len(keys)), in_=w1_words_int[:, js[0] : js[-1] + 1, :])
             for a, key in enumerate(keys):
                 w1_code[key] = tile[:, a * 2 * H : (a + 1) * 2 * H]
 
@@ -102,20 +103,16 @@ def tile_moe_pln_mlp_relu2_kernel(tc, xT, w1_words, w1_scales, w2_words, w2_scal
 
         load_w1_scales(0)
         for s in range(PASSES):
-            load_w1([(0, s), (1, s)])
-        load_w1_scales(1)
+            for e in range(2):
+                load_w1([(e, s)])
         load_w1([(e, s) for e in (2, 3) for s in range(PASSES)])
+        load_w1_scales(1)
+        load_w1([(e, s) for e in (4, 5) for s in range(PASSES)])
         load_w2_scales()
-        load_w1_scales(2)
-        load_w1([(4, s) for s in range(PASSES)])
-        load_w2(0, 4)
-        for e in range(5, E):
+        load_w2(0, 2)
+        for e in (6, 7):
             load_w1([(e, s) for s in range(PASSES)])
-        load_w2(4, E)
-
-        out_sb = sbuf([P, T], F32, "out_sb")
-        for first in range(0, T, T // 2):
-            nc.vector.memset(out_sb[:, first : first + T // 2], 0.0)
+        load_w2(2, E)
 
         gate_sb = sbuf([P, SLOTS], F32, "gate_sb")
         for half in range(2):
@@ -123,59 +120,60 @@ def tile_moe_pln_mlp_relu2_kernel(tc, xT, w1_words, w1_scales, w2_words, w2_scal
             for j in range(4):
                 column = gate_cols[:, 4 * half + j : 4 * half + j + 1].to_broadcast([P, P])
                 nc.tensor.transpose(bank[:, j * P : (j + 1) * P], column, ident[:])
-            nc.scalar.activation(
-                out=gate_sb[:].rearrange("n (p half j) -> n half p j", half=2, j=4)[:, half],
-                in_=bank[:].rearrange("n (j p) -> n p j", j=4),
-                func=ACT.Copy,
+            nc.vector.tensor_copy(
+                gate_sb[:].rearrange("n (p half j) -> n half p j", half=2, j=4)[:, half],
+                bank[:].rearrange("n (j p) -> n p j", j=4),
             )
 
         def gather(engine, dst, r, first, count):
-            window = rows[r][:].indirect(offsets[:, first // 16 : (first + count) // 16])
+            window = rows[r].indirect(offsets[:, first // 16 : (first + count) // 16])
             if engine == "scalar":
                 nc.scalar.activation(out=dst, in_=window, func=ACT.Copy)
             else:
                 nc.vector.tensor_copy(dst, window)
 
-        woven = [sbuf([P, 4 * SLOTS], BF16, f"woven{s}") for s in range(PASSES)]
-
-        def weave(u, planes, first, count):
-            s, v = divmod(u, 2)
-            dst = woven[s][:, 4 * first : 4 * (first + count)].rearrange("p (c t) -> p c t", t=4)[:, :, 2 * v : 2 * v + 2]
-            nc.vector.tensor_copy(dst, planes.rearrange("p j c -> p c j"))
+        def weave(woven, planes):
+            dst = woven.rearrange("p (c i t) -> p c t i", i=4, t=4)[:, :, : planes.shape[1], :]
+            nc.vector.tensor_copy(dst, planes.rearrange("p t (c i) -> p c t i", i=4))
 
         words, scales = {}, {}
 
-        def quantise_tokens(s, first, last, slot=None):
+        def quantise_tokens(s, first, last, woven, slot=None):
             count = C * (last - first)
             codes = sbuf([P, count], U32, f"words{s}_{first}", slot)
             scale_bytes = sbuf([P, count], U8, f"scales{s}_{first}")
-            nc.vector.quantize_mx(out=codes[:].bitcast(FP8X4), scales=scale_bytes[:], in_=woven[s][:, 4 * C * first : 4 * C * last])
+            nc.vector.quantize_mx(out=codes[:].bitcast(FP8X4), scales=scale_bytes[:], in_=woven)
             for e in range(first, last):
                 words[e, s] = codes[:, (e - first) * C : (e - first + 1) * C]
                 scales[e, s] = scale_bytes[:, (e - first) * C : (e - first + 1) * C]
 
-        planes = [sbuf([P, 2, SLOTS], BF16, f"planes{u}") for u in range(3)]
-        for u in range(2):
-            gather("scalar", planes[u][:, 0, :], 2 * u, 0, SLOTS)
-            gather("vector", planes[u][:, 1, :], 2 * u + 1, 0, SLOTS)
-            weave(u, planes[u][:], 0, SLOTS)
-        for e in range(E):
-            quantise_tokens(0, e, e + 1)
-        half = SLOTS // 2
-        gather("scalar", planes[2][:, 0, :], 4, 0, SLOTS)
-        gather("scalar", planes[2][:, 1, :half], 5, 0, half)
-        gather("vector", planes[2][:, 1, half:], 5, half, half)
-        weave(2, planes[2][:], 0, SLOTS)
-        last_planes = sbuf([P, 7 * GROUP], BF16, "last_planes")
-        blocks = last_planes[:].rearrange("p (b c) -> p b c", c=GROUP)
-        gather("scalar", last_planes[:, : 3 * GROUP], 6, 0, 3 * GROUP)
-        gather("vector", blocks[:, 3, :], 6, 3 * GROUP, GROUP)
-        for g in range(GROUPS):
-            b = max(4, g + 3)
-            gather("scalar", blocks[:, b, :], 7, g * GROUP, GROUP)
-            weave(3, blocks[:, g : b + 1 : b - g, :], g * GROUP, GROUP)
-            if g < 2:
-                quantise_tokens(1, 2 * g, 2 * g + 2)
+        planes = [sbuf([P, 4, SLOTS], dtype, f"planes{s}") for s, dtype in enumerate((F32, BF16))]
+        for r in range(6):
+            s, t = divmod(r, 4)
+            by_scalar = (SLOTS, 0, SLOTS, 0, SLOTS, 3 * GROUP)[r]
+            if by_scalar > 0:
+                gather("scalar", planes[s][:, t, :by_scalar], r, 0, by_scalar)
+            if by_scalar < SLOTS:
+                gather("vector", planes[s][:, t, by_scalar:], r, by_scalar, SLOTS - by_scalar)
+            if r == 3:
+                first_woven = sbuf([P, 4 * SLOTS], BF16, "first_woven")
+                weave(first_woven[:], planes[0][:])
+                for first, last in ((0, 2), (2, 3), (3, 4), (4, 5), (5, 8)):
+                    quantise_tokens(0, first, last, first_woven[:, 4 * C * first : 4 * C * last])
+        woven = {0: sbuf([P, 4 * GROUP], BF16, "woven0")}
+        weave(woven[0][:], planes[1][:, :2, :GROUP])
+        group0 = woven[0][:].rearrange("p (c t) -> p c t", t=4)
+        gather("vector", group0[:, :, 2], 6, 0, GROUP)
+        gather("scalar", planes[1][:, 2, GROUP:], 6, GROUP, SLOTS - GROUP)
+        gather("vector", group0[:, :, 3], 7, 0, GROUP)
+        quantise_tokens(1, 0, 2, woven[0][:])
+        for g in range(1, GROUPS):
+            cols = slice(g * GROUP, (g + 1) * GROUP)
+            gather("scalar", planes[1][:, 3, cols], 7, g * GROUP, GROUP)
+            woven[g] = sbuf([P, 4 * GROUP], BF16, f"woven{g}", f"woven{g % 2}")
+            weave(woven[g][:], planes[1][:, :, cols])
+            if g == 1:
+                quantise_tokens(1, 2, 4, woven[1][:])
 
         relued, hidden, hidden_words, hidden_scales, y_sb = {}, {}, {}, {}, {}
 
@@ -195,7 +193,7 @@ def tile_moe_pln_mlp_relu2_kernel(tc, xT, w1_words, w1_scales, w2_words, w2_scal
                 first_layer_pass(e, s)
 
         def relu(e):
-            slot = {0: "words0_2", 1: "scales0_2"}.get(e)
+            slot = {0: "words0_2", 1: "scales0_2", 5: "words0_4"}.get(e)
             relued[e] = sbuf([C, 4, P], F32, f"relued{e}", slot)
             sums = banks[SUM_BANK[e]][:].rearrange("c (p t) -> c t p", t=4)
             if e in RELU_ON_VECTOR:
@@ -218,7 +216,7 @@ def tile_moe_pln_mlp_relu2_kernel(tc, xT, w1_words, w1_scales, w2_words, w2_scal
             )
 
         def quantise_hidden(g):
-            slot = {0: "words0_4", 1: "words0_6"}.get(g)
+            slot = {0: "words0_4", 1: "h_scales0"}.get(g)
             hidden_words[g] = sbuf([P, GROUP], U32, f"h_words{g}", slot)
             hidden_scales[g] = sbuf([P, GROUP], U8, f"h_scales{g}")
             nc.vector.quantize_mx(out=hidden_words[g][:].bitcast(FP8X4), scales=hidden_scales[g][:], in_=hidden[g][:].rearrange("p c t -> p (c t)"))
@@ -239,7 +237,7 @@ def tile_moe_pln_mlp_relu2_kernel(tc, xT, w1_words, w1_scales, w2_words, w2_scal
 
         def copy_y(g):
             y_sb[g] = sbuf([P, GROUP], F32, f"y_sb{g}")
-            if g == 0:
+            if g < 2:
                 nc.vector.tensor_copy(y_sb[g][:], banks[Y_BANK[g]][:, :GROUP])
             else:
                 nc.scalar.copy(y_sb[g][:], banks[Y_BANK[g]][:, :GROUP])
@@ -255,8 +253,8 @@ def tile_moe_pln_mlp_relu2_kernel(tc, xT, w1_words, w1_scales, w2_words, w2_scal
         first_layer(3)
         for e in range(4):
             relu(e)
-        quantise_tokens(1, 4, 6, "words0_3")
-        quantise_tokens(1, 6, 8, "words1_2")
+        quantise_tokens(1, 4, 6, woven[2][:], "words0_3")
+        quantise_tokens(1, 6, 8, woven[3][:], "words1_2")
         for e in range(4):
             turn(e)
         for e in range(4):
@@ -276,11 +274,11 @@ def tile_moe_pln_mlp_relu2_kernel(tc, xT, w1_words, w1_scales, w2_words, w2_scal
         turn(5)
         first_layer(7)
         second_layer(1)
-        relu(7)
         square(4)
+        square(5)
+        relu(7)
         turn(6)
         turn(7)
-        square(5)
         copy_y(1)
         quantise_hidden(2)
         scatter(1)

@@ -107,7 +107,8 @@ def tile_moe_pln_mlp_relu2_kernel(tc, xT, w1_words, w1_scales, w2_words, w2_scal
                 load_w1([(e, s)])
         load_w1([(e, s) for e in (2, 3) for s in range(PASSES)])
         load_w1_scales(1)
-        load_w1([(e, s) for e in (4, 5) for s in range(PASSES)])
+        for e in (4, 5):
+            load_w1([(e, s) for s in range(PASSES)])
         load_w2_scales()
         load_w2(0, 2)
         for e in (6, 7):

@@ -105,7 +105,8 @@ def tile_moe_pln_mlp_relu2_kernel(tc, xT, w1_words, w1_scales, w2_words, w2_scal
         for s in range(PASSES):
             for e in range(2):
                 load_w1([(e, s)])
-        load_w1([(e, s) for e in (2, 3) for s in range(PASSES)])
+        for e in (2, 3):
+            load_w1([(e, s) for s in range(PASSES)])
         load_w1_scales(1)
         for e in (4, 5):
             load_w1([(e, s) for s in range(PASSES)])

from contextlib import ExitStack

import concourse.mybir as mybir
from concourse.masks import make_identity

K, T, E, C, H, N = 1024, 2048, 8, 128, 512, 128
SLOTS = E * C
FLOPS = 2 * SLOTS * (K * H + H * N)

F32 = mybir.dt.float32
BF16 = mybir.dt.bfloat16
I32 = mybir.dt.int32
U32 = mybir.dt.uint32
U16 = mybir.dt.uint16
U8 = mybir.dt.uint8
FP8X4 = mybir.dt.float8_e4m3fn_x4
FP4X4 = mybir.dt.float4_e2m1fn_x4
ACT = mybir.ActivationFunctionType
MULT = mybir.AluOpType.mult

P = 128
PASSES = K // 512
ROWS = 4 * PASSES
GROUP = 2 * C
GROUPS = SLOTS // GROUP

SUM_BANK = (0, 1, 2, 3, 1, 2, 3, 2)
TURNED_BANK = (4, 5, 6, 0, 7, 6, 0, 1)
Y_BANK = (7, 3, 5, 4)
GATE_BANKS = (6, 7)
RELU_ON_VECTOR = (1, 3, 4)


def tile_moe_pln_mlp_relu2_kernel(tc, xT, w1_words, w1_scales, w2_words, w2_scales, gate, offs, out):
    nc = tc.nc
    with ExitStack() as ctx:
        lists = ctx.enter_context(tc.tile_pool(name="lists", bufs=1))
        held = ctx.enter_context(tc.tile_pool(name="held", bufs=1))
        psum = ctx.enter_context(tc.psum_pool(name="psum", bufs=1))
        banks = [psum.tile([P, 512], F32, name=f"bank{b}") for b in range(8)]
        offsets = lists.tile([P, SLOTS // 16], U16, name="offsets")

        def sbuf(shape, dtype, name, slot=None):
            return held.tile(shape, dtype, name=name, tag=slot or name, align_bytes=64)

        scale_runs = ((0, 4), (4, 8))
        w1_scale_tiles = [sbuf([P, (last - first) * PASSES * H], U8, f"w1s{first}") for first, last in scale_runs]
        w1_scale = {
            (e, s): tile[:, ((e - first) * PASSES + s) * H : ((e - first) * PASSES + s + 1) * H]
            for tile, (first, last) in zip(w1_scale_tiles, scale_runs)
            for e in range(first, last)
            for s in range(PASSES)
        }
        w2_scale = sbuf([P, E * N], U8, "w2s")
        out_sb = sbuf([P, T], F32, "out_sb")
        nc.vector.memset(out_sb[:, : T // 2], 0.0)
        nc.scalar.activation(out=out_sb[:, T // 2 :], in_=out_sb[:, : T // 2], func=ACT.Copy)
        for tile in w1_scale_tiles + [w2_scale]:
            nc.vector.memset(tile[:].bitcast(I32), 0)

        gate_cols = sbuf([P, SLOTS // P], F32, "gate_cols")
        nc.scalar.dma_start(out=gate_cols[:], in_=gate[0].rearrange("(p j) -> p j", p=P))
        nc.sync.dma_start(offsets[:], offs)
        x_rows = xT.rearrange("(s p t) token -> s p (t token)", s=PASSES, t=4)
        rows = []
        for r, count in ((0, 2), (2, 2), (4, 1), (5, 1), (6, 1), (7, 1)):
            tile = sbuf([P, count * T], F32, f"row{r}")
            nc.sync.dma_start(out=tile[:], in_=x_rows[r // 4][:, (r % 4) * T : (r % 4 + count) * T])
            rows.extend(tile[:, a * T : (a + 1) * T] for a in range(count))

        ident = sbuf([P, P], F32, "ident")
        make_identity(nc, ident[:])

        w1_words_int = w1_words.bitcast(I32).rearrange("e s p b -> p (e s) b")
        w2_words_int = w2_words.bitcast(I32).rearrange("e o p b -> p (e o) b")
        w1_scales_int = w1_scales.bitcast(I32).rearrange("e s (q r) b -> r q (e s) b", r=4)
        w2_scales_int = w2_scales.bitcast(I32).rearrange("e o (q r) b -> r q (e o) b", r=4)
        w1_code, w2_code = {}, {}

        def load_w1_scales(run):
            first, last = scale_runs[run]
            dst = w1_scale_tiles[run][:].bitcast(I32).rearrange("p (j b) -> p j b", j=(last - first) * PASSES)
            for r in range(4):
                nc.sync.dma_start(out=dst[r:P:32], in_=w1_scales_int[r][:, first * PASSES : last * PASSES, :])

        def load_w2_scales():
            dst = w2_scale[:].bitcast(I32).rearrange("p (e b) -> p e b", e=E)
            for r in range(4):
                nc.sync.dma_start(out=dst[r:P:32], in_=w2_scales_int[r])

        def load_w1(keys):
            js = [PASSES * e + s for e, s in keys]
            tile = sbuf([P, len(keys) * 2 * H], U8, f"w1_{js[0]}")
            nc.sync.dma_start(out=tile[:].bitcast(I32).rearrange("p (j b) -> p j b", j=len(keys)), in_=w1_words_int[:, js[0] : js[-1] + 1, :])
            for a, key in enumerate(keys):
                w1_code[key] = tile[:, a * 2 * H : (a + 1) * 2 * H]

        def load_w2(first, last):
            tile = sbuf([P, (last - first) * 2 * N], U8, f"w2_{first}")
            nc.sync.dma_start(out=tile[:].bitcast(I32).rearrange("p (e b) -> p e b", e=last - first), in_=w2_words_int[:, first:last, :])
            for e in range(first, last):
                w2_code[e] = tile[:, (e - first) * 2 * N : (e - first + 1) * 2 * N]

        load_w1_scales(0)
        for s in range(PASSES):
            for e in range(2):
                load_w1([(e, s)])
        for e in (2, 3):
            load_w1([(e, s) for s in range(PASSES)])
        load_w1_scales(1)
        for e in (4, 5):
            load_w1([(e, s) for s in range(PASSES)])
        load_w2_scales()
        load_w2(0, 2)
        for e in (6, 7):
            load_w1([(e, s) for s in range(PASSES)])
        load_w2(2, E)

        gate_sb = sbuf([P, SLOTS], F32, "gate_sb")
        for half in range(2):
            bank = banks[GATE_BANKS[half]]
            for j in range(4):
                column = gate_cols[:, 4 * half + j : 4 * half + j + 1].to_broadcast([P, P])
                nc.tensor.transpose(bank[:, j * P : (j + 1) * P], column, ident[:])
            nc.vector.tensor_copy(
                gate_sb[:].rearrange("n (p half j) -> n half p j", half=2, j=4)[:, half],
                bank[:].rearrange("n (j p) -> n p j", j=4),
            )

        def gather(engine, dst, r, first, count):
            window = rows[r].indirect(offsets[:, first // 16 : (first + count) // 16])
            if engine == "scalar":
                nc.scalar.activation(out=dst, in_=window, func=ACT.Copy)
            else:
                nc.vector.tensor_copy(dst, window)

        def weave(woven, planes):
            dst = woven.rearrange("p (c i t) -> p c t i", i=4, t=4)[:, :, : planes.shape[1], :]
            nc.vector.tensor_copy(dst, planes.rearrange("p t (c i) -> p c t i", i=4))

        words, scales = {}, {}

        def quantise_tokens(s, first, last, woven, slot=None):
            count = C * (last - first)
            codes = sbuf([P, count], U32, f"words{s}_{first}", slot)
            scale_bytes = sbuf([P, count], U8, f"scales{s}_{first}")
            nc.vector.quantize_mx(out=codes[:].bitcast(FP8X4), scales=scale_bytes[:], in_=woven)
            for e in range(first, last):
                words[e, s] = codes[:, (e - first) * C : (e - first + 1) * C]
                scales[e, s] = scale_bytes[:, (e - first) * C : (e - first + 1) * C]

        planes = [sbuf([P, 4, SLOTS], dtype, f"planes{s}") for s, dtype in enumerate((F32, BF16))]
        for r in range(6):
            s, t = divmod(r, 4)
            by_scalar = (SLOTS, 0, SLOTS, 0, SLOTS, 3 * GROUP)[r]
            if by_scalar > 0:
                gather("scalar", planes[s][:, t, :by_scalar], r, 0, by_scalar)
            if by_scalar < SLOTS:
                gather("vector", planes[s][:, t, by_scalar:], r, by_scalar, SLOTS - by_scalar)
            if r == 3:
                first_woven = sbuf([P, 4 * SLOTS], BF16, "first_woven")
                weave(first_woven[:], planes[0][:])
                for first, last in ((0, 2), (2, 3), (3, 4), (4, 5), (5, 8)):
                    quantise_tokens(0, first, last, first_woven[:, 4 * C * first : 4 * C * last])
        woven = {0: sbuf([P, 4 * GROUP], BF16, "woven0")}
        weave(woven[0][:], planes[1][:, :2, :GROUP])
        group0 = woven[0][:].rearrange("p (c t) -> p c t", t=4)
        gather("vector", group0[:, :, 2], 6, 0, GROUP)
        gather("scalar", planes[1][:, 2, GROUP:], 6, GROUP, SLOTS - GROUP)
        gather("vector", group0[:, :, 3], 7, 0, GROUP)
        quantise_tokens(1, 0, 2, woven[0][:])
        for g in range(1, GROUPS):
            cols = slice(g * GROUP, (g + 1) * GROUP)
            gather("scalar", planes[1][:, 3, cols], 7, g * GROUP, GROUP)
            woven[g] = sbuf([P, 4 * GROUP], BF16, f"woven{g}", f"woven{g % 2}")
            weave(woven[g][:], planes[1][:, :, cols])
            if g == 1:
                quantise_tokens(1, 2, 4, woven[1][:])

        relued, hidden, hidden_words, hidden_scales, y_sb = {}, {}, {}, {}, {}

        def first_layer_pass(e, s):
            nc.tensor.matmul_mx(
                out=banks[SUM_BANK[e]][:],
                lhsT=words[e, s].bitcast(FP8X4),
                lhsT_scale=scales[e, s],
                rhs=w1_code[e, s].bitcast(FP4X4),
                rhs_scale=w1_scale[e, s],
                start=(s == 0),
                stop=(s == PASSES - 1),
            )

        def first_layer(e):
            for s in range(PASSES):
                first_layer_pass(e, s)

        def relu(e):
            slot = {0: "words0_2", 1: "scales0_2", 5: "words0_4"}.get(e)
            relued[e] = sbuf([C, 4, P], F32, f"relued{e}", slot)
            sums = banks[SUM_BANK[e]][:].rearrange("c (p t) -> c t p", t=4)
            if e in RELU_ON_VECTOR:
                nc.vector.tensor_scalar_max(relued[e][:], sums, 0.0)
            else:
                nc.scalar.activation(out=relued[e][:], in_=sums, func=ACT.Relu)

        def turn(e):
            for t in range(4):
                nc.tensor.transpose(banks[TURNED_BANK[e]][:, t * C : (t + 1) * C], relued[e][:, t, :], ident[:])

        def square(e):
            g, side = divmod(e, 2)
            if side == 0:
                hidden[g] = sbuf([P, GROUP, 4], BF16, f"hidden{g}")
            nc.scalar.activation(
                out=hidden[g][:, side * C : (side + 1) * C, :],
                in_=banks[TURNED_BANK[e]][:].rearrange("p (t c) -> p c t", t=4),
                func=ACT.Square,
            )

        def quantise_hidden(g):
            slot = {0: "words0_4", 1: "h_scales0"}.get(g)
            hidden_words[g] = sbuf([P, GROUP], U32, f"h_words{g}", slot)
            hidden_scales[g] = sbuf([P, GROUP], U8, f"h_scales{g}")
            nc.vector.quantize_mx(out=hidden_words[g][:].bitcast(FP8X4), scales=hidden_scales[g][:], in_=hidden[g][:].rearrange("p c t -> p (c t)"))

        def second_layer(g):
            for side in range(2):
                e = 2 * g + side
                cols = slice(side * C, (side + 1) * C)
                nc.tensor.matmul_mx(
                    out=banks[Y_BANK[g]][:, cols],
                    lhsT=w2_code[e].bitcast(FP4X4),
                    lhsT_scale=w2_scale[:, e * N : (e + 1) * N],
                    rhs=hidden_words[g][:, cols].bitcast(FP8X4),
                    rhs_scale=hidden_scales[g][:, cols],
                    start=True,
                    stop=True,
                )

        def copy_y(g):
            y_sb[g] = sbuf([P, GROUP], F32, f"y_sb{g}")
            if g < 2:
                nc.vector.tensor_copy(y_sb[g][:], banks[Y_BANK[g]][:, :GROUP])
            else:
                nc.scalar.copy(y_sb[g][:], banks[Y_BANK[g]][:, :GROUP])

        def scatter(g):
            picked = offsets[:, g * GROUP // 16 : (g + 1) * GROUP // 16]
            nc.vector.tensor_tensor(out_sb[:].indirect(picked), y_sb[g][:], gate_sb[:, g * GROUP : (g + 1) * GROUP], MULT)

        for s in range(PASSES):
            for e in range(2):
                first_layer_pass(e, s)
        first_layer(2)
        first_layer(3)
        for e in range(4):
            relu(e)
        quantise_tokens(1, 4, 6, woven[2][:], "words0_3")
        quantise_tokens(1, 6, 8, woven[3][:], "words1_2")
        for e in range(4):
            turn(e)
        for e in range(4):
            square(e)
        first_layer(4)
        first_layer(5)
        quantise_hidden(0)
        second_layer(0)
        first_layer(6)
        relu(4)
        copy_y(0)
        quantise_hidden(1)
        scatter(0)
        relu(5)
        relu(6)
        turn(4)
        turn(5)
        first_layer(7)
        second_layer(1)
        square(4)
        square(5)
        relu(7)
        turn(6)
        turn(7)
        copy_y(1)
        quantise_hidden(2)
        scatter(1)
        square(6)
        square(7)
        second_layer(2)
        quantise_hidden(3)
        copy_y(2)
        second_layer(3)
        copy_y(3)
        scatter(2)
        scatter(3)
        nc.sync.dma_start(out=out, in_=out_sb[:])
